import numpy as np
import ml_dtypes


def mxq(x, axis, fmt="e4m3"):
    dtype, down = {"e4m3": (ml_dtypes.float8_e4m3fn, 7), "e5m2": (ml_dtypes.float8_e5m2, 14)}[fmt]
    v = np.moveaxis(np.asarray(x, np.float32).astype(ml_dtypes.bfloat16).astype(np.float64), axis, -1)
    blocks = v.reshape(v.shape[:-1] + (-1, 32))
    amax = np.abs(blocks).max(-1, keepdims=True)
    byte = np.maximum(np.where(amax > 0, np.frexp(amax)[1] - 1 + 127, 0) - down, 1)
    scale = np.exp2(byte - 127.0)
    codes = (blocks / scale).astype(np.float32).astype(dtype).astype(np.float64)
    return np.moveaxis((codes * scale).reshape(v.shape), -1, axis)


WIDE = False


def mx_kscale(k):
    if not WIDE:
        return np.ones(k)
    levels = np.array([10, -10, 5, -5, 0])
    if k % 512:
        return np.exp2(np.random.permutation(np.resize(levels, k // 32))).repeat(32)
    a = np.empty((k // 512, 16))
    for p in range(k // 512):
        a[p, :8] = np.random.permutation(np.resize(levels, 8))
        for g in range(8):
            far = levels[np.abs(levels - a[p, g]) >= 10]
            a[p, g + 8] = far[np.random.randint(len(far))]
    return np.exp2(a.ravel()).repeat(32)


def f64(x):
    return np.asarray(x).astype(np.float64)


def striped(idx):
    return np.tile(idx.reshape(-1, 16).T, (8, 1)).astype(np.uint16)


def unstriped(offs):
    return offs[:16].T.reshape(-1).astype(np.int64)


def pack_weight(w):
    k, n = w.shape
    w = f64(np.asarray(w, np.float32).astype(ml_dtypes.bfloat16)).reshape(k // 32, 32, n)
    amax = np.abs(w).max(1)
    byte = np.clip(np.where(amax > 0, np.frexp(amax)[1] - 1 + 127 - 7, 1), 1, 254)
    scaled = (w * np.exp2(127.0 - byte)[:, None, :]).reshape(k, n).astype(np.float32)
    words = np.ascontiguousarray(scaled.reshape(k // 512, 128, 4, n).transpose(0, 1, 3, 2)).astype(ml_dtypes.float8_e4m3fn).view(np.uint8)
    return words, np.ascontiguousarray(byte.astype(np.uint8).reshape(k // 512, 16, n))


def unpack_weight(words, scales):
    g, p, n, _ = words.shape
    vals = np.ascontiguousarray(words).view(ml_dtypes.float8_e4m3fn).astype(np.float64) * np.repeat(np.exp2(scales.astype(np.float64) - 127.0), 8, axis=1)[..., None]
    return vals.transpose(0, 1, 3, 2).reshape(g * 512, n)


def gelu(v):
    return 0.5 * v * (1.0 + np.tanh(np.sqrt(2.0 / np.pi) * (v + 0.044715 * v**3)))


K, T, S, N, U = 512, 2048, 1024, 256, 2048
P = 2 ** 7


def setup_inputs():
    n = np.random.standard_normal
    s = mx_kscale(K)[:, None]
    packed_xT = pack_weight(n((K, T)) * s)
    return {
        "x_words": packed_xT[0],
        "x_scales": packed_xT[1],
        "gate": np.tile(np.random.uniform(0.5, 1.5, S), (P, 1)).astype(np.float32),
        "w1": (n((K, N)) / np.sqrt(K) / s).astype(np.float32),
        "offs": striped(np.random.permutation(T)[:S]),
        "dst": striped(np.random.permutation(U)[:S]),
    }


def reference(x_words, x_scales, gate, w1, offs, dst):
    xq = unpack_weight(x_words, x_scales)[:, unstriped(offs)]
    y = gelu(mxq(f64(w1), 0, "e4m3").T @ xq)
    out = np.zeros((N, U))
    out[:, unstriped(dst)] = y * f64(gate)[:1]
    return out

@@ -1,0 +1,109 @@
+from contextlib import ExitStack
+
+import concourse.mybir as mybir
+
+K, T, S, N, U = 512, 2048, 1024, 256, 2048
+FLOPS = 2 * K * N * S
+
+F32 = mybir.dt.float32
+BF16 = mybir.dt.bfloat16
+I32 = mybir.dt.int32
+U32 = mybir.dt.uint32
+U16 = mybir.dt.uint16
+U8 = mybir.dt.uint8
+FP8X4 = mybir.dt.float8_e4m3fn_x4
+GELU = mybir.ActivationFunctionType.Gelu_apprx_tanh
+MULT = mybir.AluOpType.mult
+
+P = 128
+PACK = 4
+LANES = 16
+HALF = S // 2
+
+
+def tile_picked_route2_lingelu_p_kernel(tc, x_words, x_scales, gate, w1, offs, dst, out):
+    nc = tc.nc
+    with ExitStack() as ctx:
+        keep = ctx.enter_context(tc.tile_pool(name="keep", bufs=1))
+        psum = ctx.enter_context(tc.psum_pool(name="psum", bufs=1))
+
+        pick = keep.tile([P, S // LANES], U16, name="pick")
+        place = keep.tile([P, S // LANES], U16, name="place")
+        words = keep.tile([P, T], U32, name="words", align_bytes=64)
+        scales = keep.tile([P, T], U8, name="scales", align_bytes=64)
+        picked_words = keep.tile([P, S], U32, name="picked_words", align_bytes=64)
+        picked_scales = keep.tile([P, S], U8, name="picked_scales", align_bytes=64)
+        w_raw = [keep.tile([P, PACK, P], F32, name="w_raw%d" % b) for b in range(2)]
+        w_bf = [keep.tile([P, P, PACK], BF16, name="w_bf%d" % b, align_bytes=64) for b in range(2)]
+        w_words = [keep.tile([P, P], U32, name="w_words%d" % b, align_bytes=64) for b in range(2)]
+        w_scales = [keep.tile([P, P], U8, name="w_scales%d" % b, align_bytes=64) for b in range(2)]
+        gates = keep.tile([P, S], F32, name="gates")
+        y = [keep.tile([P, S], F32, name="y%d" % b) for b in range(2)]
+        window = [keep.tile([P, U], F32, name="window%d" % b) for b in range(2)]
+
+        w_rows = w1.rearrange("(p j) m -> p j m", j=PACK)
+
+        def entries(tile, a, b):
+            return tile[:, a // LANES : b // LANES]
+
+        def quantize(b):
+            nc.scalar.copy(w_bf[b][:], w_raw[b][:].rearrange("p j m -> p m j"))
+            nc.vector.quantize_mx(
+                out=w_words[b][:].bitcast(FP8X4),
+                scales=w_scales[b][:],
+                in_=w_bf[b][:].rearrange("p m j -> p (m j)"),
+            )
+
+        def gather_words(a, b):
+            nc.vector.tensor_copy(picked_words[:, a:b], words[:].indirect(entries(pick, a, b)))
+
+        def layer(blk, a, b):
+            acc = psum.tile([P, b - a], F32, name="acc%d_%d" % (blk, a))
+            nc.tensor.matmul_mx(
+                out=acc[:],
+                lhsT=w_words[blk][:].bitcast(FP8X4),
+                lhsT_scale=w_scales[blk][:],
+                rhs=picked_words[:, a:b].bitcast(FP8X4),
+                rhs_scale=picked_scales[:, a:b],
+                start=True,
+                stop=True,
+            )
+            nc.scalar.activation(y[blk][:, a:b], acc[:], GELU)
+
+        def scatter(blk, a, b):
+            nc.vector.tensor_tensor(
+                window[blk][:].indirect(entries(place, a, b)), y[blk][:, a:b], gates[:, a:b], MULT
+            )
+
+        XA = 512
+        x_flat = x_words[0].rearrange("p n t -> p (n t)").bitcast(I32)
+        nc.vector.memset(scales[:].bitcast(I32), 0)
+        nc.sync.dma_start(pick[:], offs)
+        nc.sync.dma_start(words[:, :XA].bitcast(I32), x_flat[:, :XA])
+        for r in range(4):
+            nc.sync.dma_start(scales[r:P:32, :].bitcast(I32), x_scales[0, r:16:4, :].bitcast(I32))
+        nc.sync.dma_start(w_raw[0][:], w_rows[:, :, 0:P])
+        nc.sync.dma_start(words[:, XA:].bitcast(I32), x_flat[:, XA:])
+        nc.sync.dma_start(w_raw[1][:], w_rows[:, :, P:N])
+        nc.sync.dma_start(gates[:, :HALF], gate[:, :HALF])
+        nc.sync.dma_start(place[:], dst)
+        nc.sync.dma_start(gates[:, HALF:], gate[:, HALF:])
+
+        nc.vector.memset(window[0][:], 0.0)
+        nc.vector.memset(window[1][:, :1024], 0.0)
+        nc.scalar.activation(window[1][:, 1024:1536], window[0][:, 1024:1536], GELU)
+
+        nc.vector.tensor_copy(picked_scales[:], scales[:].indirect(pick[:]))
+        quantize(0)
+        nc.scalar.activation(window[1][:, 1536:], window[0][:, 1536:], GELU)
+        for a, b in ((0, 256), (256, 512), (512, 1024)):
+            gather_words(a, b)
+            layer(0, a, b)
+        quantize(1)
+        scatter(0, 0, HALF)
+        scatter(0, HALF, S)
+        nc.sync.dma_start(out[0:P, :], window[0][:])
+        layer(1, 0, HALF)
+        layer(1, HALF, S)
+        scatter(1, 0, S)
+        nc.sync.dma_start(out[P:N, :], window[1][:])

@@ -75,13 +75,14 @@ def tile_picked_route2_lingelu_p_kernel(tc, x_words, x_scales, gate, w1, offs, d
                 window[blk][:].indirect(entries(place, a, b)), y[blk][:, a:b], gates[:, a:b], MULT
             )
 
-        XA = 512
+        XA = 256
         x_flat = x_words[0].rearrange("p n t -> p (n t)").bitcast(I32)
         nc.vector.memset(scales[:].bitcast(I32), 0)
         nc.sync.dma_start(pick[:], offs)
         nc.sync.dma_start(words[:, :XA].bitcast(I32), x_flat[:, :XA])
         for r in range(4):
-            nc.sync.dma_start(scales[r:P:32, :].bitcast(I32), x_scales[0, r:16:4, :].bitcast(I32))
+            queue = nc.sync if r < 2 else nc.scalar
+            queue.dma_start(scales[r:P:32, :].bitcast(I32), x_scales[0, r:16:4, :].bitcast(I32))
         nc.sync.dma_start(w_raw[0][:], w_rows[:, :, 0:P])
         nc.sync.dma_start(words[:, XA:].bitcast(I32), x_flat[:, XA:])
         nc.sync.dma_start(w_raw[1][:], w_rows[:, :, P:N])
@@ -90,20 +91,23 @@ def tile_picked_route2_lingelu_p_kernel(tc, x_words, x_scales, gate, w1, offs, d
         nc.sync.dma_start(gates[:, HALF:], gate[:, HALF:])
 
         nc.vector.memset(window[0][:], 0.0)
-        nc.vector.memset(window[1][:, :1024], 0.0)
-        nc.scalar.activation(window[1][:, 1024:1536], window[0][:, 1024:1536], GELU)
+        for c in range(0, U // 2, 512):
+            nc.scalar.activation(window[1][:, c : c + 512], window[0][:, c : c + 512], GELU)
 
         nc.vector.tensor_copy(picked_scales[:], scales[:].indirect(pick[:]))
         quantize(0)
-        nc.scalar.activation(window[1][:, 1536:], window[0][:, 1536:], GELU)
-        for a, b in ((0, 256), (256, 512), (512, 1024)):
+        for c in range(U // 2, U, 512):
+            nc.scalar.activation(window[1][:, c : c + 512], window[0][:, c : c + 512], GELU)
+        for a, b in ((0, 256), (256, 512)):
             gather_words(a, b)
             layer(0, a, b)
+        gather_words(HALF, S)
         quantize(1)
         scatter(0, 0, HALF)
-        scatter(0, HALF, S)
-        nc.sync.dma_start(out[0:P, :], window[0][:])
         layer(1, 0, HALF)
         layer(1, HALF, S)
         scatter(1, 0, S)
         nc.sync.dma_start(out[P:N, :], window[1][:])
+        layer(0, HALF, S)
+        scatter(0, HALF, S)
+        nc.sync.dma_start(out[0:P, :], window[0][:])

@@ -19,6 +19,8 @@ P = 128
 PACK = 4
 LANES = 16
 HALF = S // 2
+XA = 256
+PIECES = ((0, 256), (256, 768), (768, 1024))
 
 
 def tile_picked_route2_lingelu_p_kernel(tc, x_words, x_scales, gate, w1, offs, dst, out):
@@ -33,36 +35,23 @@ def tile_picked_route2_lingelu_p_kernel(tc, x_words, x_scales, gate, w1, offs, d
         scales = keep.tile([P, T], U8, name="scales", align_bytes=64)
         picked_words = keep.tile([P, S], U32, name="picked_words", align_bytes=64)
         picked_scales = keep.tile([P, S], U8, name="picked_scales", align_bytes=64)
-        w_raw = [keep.tile([P, PACK, P], F32, name="w_raw%d" % b) for b in range(2)]
-        w_bf = [keep.tile([P, P, PACK], BF16, name="w_bf%d" % b, align_bytes=64) for b in range(2)]
-        w_words = [keep.tile([P, P], U32, name="w_words%d" % b, align_bytes=64) for b in range(2)]
-        w_scales = [keep.tile([P, P], U8, name="w_scales%d" % b, align_bytes=64) for b in range(2)]
+        w_raw = keep.tile([P, PACK, N], F32, name="w_raw")
+        w_bf = keep.tile([P, N, PACK], BF16, name="w_bf", align_bytes=64)
+        w_words = keep.tile([P, N], U32, name="w_words", align_bytes=64)
+        w_scales = keep.tile([P, N], U8, name="w_scales", align_bytes=64)
         gates = keep.tile([P, S], F32, name="gates")
         y = [keep.tile([P, S], F32, name="y%d" % b) for b in range(2)]
         window = [keep.tile([P, U], F32, name="window%d" % b) for b in range(2)]
 
-        w_rows = w1.rearrange("(p j) m -> p j m", j=PACK)
-
         def entries(tile, a, b):
             return tile[:, a // LANES : b // LANES]
-
-        def quantize(b):
-            nc.scalar.copy(w_bf[b][:], w_raw[b][:].rearrange("p j m -> p m j"))
-            nc.vector.quantize_mx(
-                out=w_words[b][:].bitcast(FP8X4),
-                scales=w_scales[b][:],
-                in_=w_bf[b][:].rearrange("p m j -> p (m j)"),
-            )
-
-        def gather_words(a, b):
-            nc.vector.tensor_copy(picked_words[:, a:b], words[:].indirect(entries(pick, a, b)))
 
         def layer(blk, a, b):
             acc = psum.tile([P, b - a], F32, name="acc%d_%d" % (blk, a))
             nc.tensor.matmul_mx(
                 out=acc[:],
-                lhsT=w_words[blk][:].bitcast(FP8X4),
-                lhsT_scale=w_scales[blk][:],
+                lhsT=w_words[:, blk * P : (blk + 1) * P].bitcast(FP8X4),
+                lhsT_scale=w_scales[:, blk * P : (blk + 1) * P],
                 rhs=picked_words[:, a:b].bitcast(FP8X4),
                 rhs_scale=picked_scales[:, a:b],
                 start=True,
@@ -75,39 +64,40 @@ def tile_picked_route2_lingelu_p_kernel(tc, x_words, x_scales, gate, w1, offs, d
                 window[blk][:].indirect(entries(place, a, b)), y[blk][:, a:b], gates[:, a:b], MULT
             )
 
-        XA = 256
         x_flat = x_words[0].rearrange("p n t -> p (n t)").bitcast(I32)
         nc.vector.memset(scales[:].bitcast(I32), 0)
         nc.sync.dma_start(pick[:], offs)
         nc.sync.dma_start(words[:, :XA].bitcast(I32), x_flat[:, :XA])
         for r in range(4):
-            queue = nc.sync if r < 2 else nc.scalar
-            queue.dma_start(scales[r:P:32, :].bitcast(I32), x_scales[0, r:16:4, :].bitcast(I32))
-        nc.sync.dma_start(w_raw[0][:], w_rows[:, :, 0:P])
+            nc.sync.dma_start(scales[r:P:32, :].bitcast(I32), x_scales[0, r:16:4, :].bitcast(I32))
+        nc.sync.dma_start(w_raw[:], w1.rearrange("(p j) m -> p j m", j=PACK))
         nc.sync.dma_start(words[:, XA:].bitcast(I32), x_flat[:, XA:])
-        nc.sync.dma_start(w_raw[1][:], w_rows[:, :, P:N])
-        nc.sync.dma_start(gates[:, :HALF], gate[:, :HALF])
+        nc.sync.dma_start(gates[:], gate)
         nc.sync.dma_start(place[:], dst)
-        nc.sync.dma_start(gates[:, HALF:], gate[:, HALF:])
 
         nc.vector.memset(window[0][:], 0.0)
-        for c in range(0, U // 2, 512):
-            nc.scalar.activation(window[1][:, c : c + 512], window[0][:, c : c + 512], GELU)
+        nc.vector.memset(window[1][:, : U // 2], 0.0)
+        nc.scalar.activation(window[1][:, U // 2 :], window[0][:, U // 2 :], GELU)
 
         nc.vector.tensor_copy(picked_scales[:], scales[:].indirect(pick[:]))
-        quantize(0)
-        for c in range(U // 2, U, 512):
-            nc.scalar.activation(window[1][:, c : c + 512], window[0][:, c : c + 512], GELU)
-        for a, b in ((0, 256), (256, 512)):
-            gather_words(a, b)
-            layer(0, a, b)
-        gather_words(HALF, S)
-        quantize(1)
-        scatter(0, 0, HALF)
-        layer(1, 0, HALF)
-        layer(1, HALF, S)
+        nc.scalar.copy(
+            w_bf[:].rearrange("p (c i) j -> p c j i", i=4),
+            w_raw[:].rearrange("p j (c i) -> p c j i", i=4),
+        )
+        nc.vector.quantize_mx(
+            out=w_words[:].bitcast(FP8X4), scales=w_scales[:], in_=w_bf[:].rearrange("p m j -> p (m j)")
+        )
+
+        for a, b in PIECES:
+            nc.vector.tensor_copy(picked_words[:, a:b], words[:].indirect(entries(pick, a, b)))
+        first = PIECES[0][1]
+        layer(0, 0, first)
+        scatter(0, 0, first)
+        for a, b in PIECES:
+            layer(1, a, b)
         scatter(1, 0, S)
         nc.sync.dma_start(out[P:N, :], window[1][:])
-        layer(0, HALF, S)
-        scatter(0, HALF, S)
+        for a, b in PIECES[1:]:
+            layer(0, a, b)
+        scatter(0, first, S)
         nc.sync.dma_start(out[0:P, :], window[0][:])

@@ -18,9 +18,10 @@ MULT = mybir.AluOpType.mult
 P = 128
 PACK = 4
 LANES = 16
-HALF = S // 2
 XA = 256
-PIECES = ((0, 256), (256, 768), (768, 1024))
+HALF = S // 2
+FIRST = 256
+PIECES = ((0, FIRST), (FIRST, HALF), (HALF, S))
 
 
 def tile_picked_route2_lingelu_p_kernel(tc, x_words, x_scales, gate, w1, offs, dst, out):
@@ -33,26 +34,41 @@ def tile_picked_route2_lingelu_p_kernel(tc, x_words, x_scales, gate, w1, offs, d
         place = keep.tile([P, S // LANES], U16, name="place")
         words = keep.tile([P, T], U32, name="words", align_bytes=64)
         scales = keep.tile([P, T], U8, name="scales", align_bytes=64)
-        picked_words = keep.tile([P, S], U32, name="picked_words", align_bytes=64)
         picked_scales = keep.tile([P, S], U8, name="picked_scales", align_bytes=64)
-        w_raw = keep.tile([P, PACK, N], F32, name="w_raw")
-        w_bf = keep.tile([P, N, PACK], BF16, name="w_bf", align_bytes=64)
-        w_words = keep.tile([P, N], U32, name="w_words", align_bytes=64)
-        w_scales = keep.tile([P, N], U8, name="w_scales", align_bytes=64)
+        w_raw = [
+            keep.tile([P, PACK, P], F32, name="w_raw0", tag="shared", align_bytes=64),
+            keep.tile([P, PACK, P], F32, name="w_raw1"),
+        ]
+        w_bf = [keep.tile([P, P, PACK], BF16, name="w_bf%d" % b, align_bytes=64) for b in range(2)]
+        w_words = [keep.tile([P, P], U32, name="w_words%d" % b, align_bytes=64) for b in range(2)]
+        w_scales = [keep.tile([P, P], U8, name="w_scales%d" % b, align_bytes=64) for b in range(2)]
         gates = keep.tile([P, S], F32, name="gates")
         y = [keep.tile([P, S], F32, name="y%d" % b) for b in range(2)]
         window = [keep.tile([P, U], F32, name="window%d" % b) for b in range(2)]
+        picked_words = [keep.tile([P, HALF], U32, name="picked_words0", align_bytes=64)]
 
         def entries(tile, a, b):
             return tile[:, a // LANES : b // LANES]
 
+        def quantise(blk):
+            nc.scalar.copy(
+                w_bf[blk][:].rearrange("p (c i) j -> p c j i", i=4),
+                w_raw[blk][:].rearrange("p j (c i) -> p c j i", i=4),
+            )
+            nc.vector.quantize_mx(
+                out=w_words[blk][:].bitcast(FP8X4),
+                scales=w_scales[blk][:],
+                in_=w_bf[blk][:].rearrange("p m j -> p (m j)"),
+            )
+
         def layer(blk, a, b):
             acc = psum.tile([P, b - a], F32, name="acc%d_%d" % (blk, a))
+            h = a // HALF
             nc.tensor.matmul_mx(
                 out=acc[:],
-                lhsT=w_words[:, blk * P : (blk + 1) * P].bitcast(FP8X4),
-                lhsT_scale=w_scales[:, blk * P : (blk + 1) * P],
-                rhs=picked_words[:, a:b].bitcast(FP8X4),
+                lhsT=w_words[blk][:].bitcast(FP8X4),
+                lhsT_scale=w_scales[blk][:],
+                rhs=picked_words[h][:, a - h * HALF : b - h * HALF].bitcast(FP8X4),
                 rhs_scale=picked_scales[:, a:b],
                 start=True,
                 stop=True,
@@ -65,39 +81,33 @@ def tile_picked_route2_lingelu_p_kernel(tc, x_words, x_scales, gate, w1, offs, d
             )
 
         x_flat = x_words[0].rearrange("p n t -> p (n t)").bitcast(I32)
+        w_rows = w1.rearrange("(p j) m -> p j m", j=PACK)
         nc.vector.memset(scales[:].bitcast(I32), 0)
         nc.sync.dma_start(pick[:], offs)
         nc.sync.dma_start(words[:, :XA].bitcast(I32), x_flat[:, :XA])
         for r in range(4):
             nc.sync.dma_start(scales[r:P:32, :].bitcast(I32), x_scales[0, r:16:4, :].bitcast(I32))
-        nc.sync.dma_start(w_raw[:], w1.rearrange("(p j) m -> p j m", j=PACK))
         nc.sync.dma_start(words[:, XA:].bitcast(I32), x_flat[:, XA:])
-        nc.sync.dma_start(gates[:], gate)
+        for blk in range(2):
+            nc.sync.dma_start(w_raw[blk][:], w_rows[:, :, blk * P : (blk + 1) * P])
         nc.sync.dma_start(place[:], dst)
+        nc.sync.dma_start(gates[:], gate)
 
         nc.vector.memset(window[0][:], 0.0)
-        nc.vector.memset(window[1][:, : U // 2], 0.0)
-        nc.scalar.activation(window[1][:, U // 2 :], window[0][:, U // 2 :], GELU)
+        nc.scalar.activation(window[1][:], window[0][:], GELU)
 
         nc.vector.tensor_copy(picked_scales[:], scales[:].indirect(pick[:]))
-        nc.scalar.copy(
-            w_bf[:].rearrange("p (c i) j -> p c j i", i=4),
-            w_raw[:].rearrange("p j (c i) -> p c j i", i=4),
-        )
-        nc.vector.quantize_mx(
-            out=w_words[:].bitcast(FP8X4), scales=w_scales[:], in_=w_bf[:].rearrange("p m j -> p (m j)")
-        )
+        nc.vector.tensor_copy(picked_words[0][:], words[:].indirect(entries(pick, 0, HALF)))
+        quantise(0)
+        picked_words.append(keep.tile([P, HALF], U32, name="picked_words1", tag="shared", align_bytes=64))
+        nc.vector.tensor_copy(picked_words[1][:], words[:].indirect(entries(pick, HALF, S)))
+        quantise(1)
 
-        for a, b in PIECES:
-            nc.vector.tensor_copy(picked_words[:, a:b], words[:].indirect(entries(pick, a, b)))
-        first = PIECES[0][1]
-        layer(0, 0, first)
-        scatter(0, 0, first)
-        for a, b in PIECES:
-            layer(1, a, b)
-        scatter(1, 0, S)
-        nc.sync.dma_start(out[P:N, :], window[1][:])
-        for a, b in PIECES[1:]:
-            layer(0, a, b)
-        scatter(0, first, S)
-        nc.sync.dma_start(out[0:P, :], window[0][:])
+        for blk in range(2):
+            layer(blk, 0, FIRST)
+            scatter(blk, 0, FIRST)
+        for blk in range(2):
+            for a, b in PIECES[1:]:
+                layer(blk, a, b)
+            scatter(blk, FIRST, S)
+            nc.sync.dma_start(out[blk * P : (blk + 1) * P, :], window[blk][:])

@@ -18,7 +18,8 @@ MULT = mybir.AluOpType.mult
 P = 128
 PACK = 4
 LANES = 16
-XA = 256
+ROWS = 16
+BASE = P - ROWS
 HALF = S // 2
 FIRST = 256
 PIECES = ((0, FIRST), (FIRST, HALF), (HALF, S))
@@ -35,11 +36,13 @@ def tile_picked_route2_lingelu_p_kernel(tc, x_words, x_scales, gate, w1, offs, d
         words = keep.tile([P, T], U32, name="words", align_bytes=64)
         scales = keep.tile([P, T], U8, name="scales", align_bytes=64)
         picked_scales = keep.tile([P, S], U8, name="picked_scales", align_bytes=64)
+        plane = [keep.tile([P, HALF], U8, name="plane0", align_bytes=64)]
+        zero = keep.tile([P, 1], F32, name="zero")
         w_raw = [
             keep.tile([P, PACK, P], F32, name="w_raw0", tag="shared", align_bytes=64),
             keep.tile([P, PACK, P], F32, name="w_raw1"),
         ]
-        w_bf = [keep.tile([P, P, PACK], BF16, name="w_bf%d" % b, align_bytes=64) for b in range(2)]
+        w_bf = [keep.tile([P, P, PACK], BF16, name="w_bf%d" % b, tag="w_bf%d" % b, align_bytes=64) for b in range(2)]
         w_words = [keep.tile([P, P], U32, name="w_words%d" % b, align_bytes=64) for b in range(2)]
         w_scales = [keep.tile([P, P], U8, name="w_scales%d" % b, align_bytes=64) for b in range(2)]
         gates = keep.tile([P, S], F32, name="gates")
@@ -69,7 +72,7 @@ def tile_picked_route2_lingelu_p_kernel(tc, x_words, x_scales, gate, w1, offs, d
                 lhsT=w_words[blk][:].bitcast(FP8X4),
                 lhsT_scale=w_scales[blk][:],
                 rhs=picked_words[h][:, a - h * HALF : b - h * HALF].bitcast(FP8X4),
-                rhs_scale=picked_scales[:, a:b],
+                rhs_scale=plane[h][:, a - h * HALF : b - h * HALF],
                 start=True,
                 stop=True,
             )
@@ -82,32 +85,45 @@ def tile_picked_route2_lingelu_p_kernel(tc, x_words, x_scales, gate, w1, offs, d
 
         x_flat = x_words[0].rearrange("p n t -> p (n t)").bitcast(I32)
         w_rows = w1.rearrange("(p j) m -> p j m", j=PACK)
-        nc.vector.memset(scales[:].bitcast(I32), 0)
         nc.sync.dma_start(pick[:], offs)
-        nc.sync.dma_start(words[:, :XA].bitcast(I32), x_flat[:, :XA])
-        for r in range(4):
-            nc.sync.dma_start(scales[r:P:32, :].bitcast(I32), x_scales[0, r:16:4, :].bitcast(I32))
-        nc.sync.dma_start(words[:, XA:].bitcast(I32), x_flat[:, XA:])
+        nc.sync.dma_start(scales[BASE:P, :].bitcast(I32), x_scales[0].bitcast(I32))
+        nc.sync.dma_start(words[:].bitcast(I32), x_flat)
         for blk in range(2):
             nc.sync.dma_start(w_raw[blk][:], w_rows[:, :, blk * P : (blk + 1) * P])
         nc.sync.dma_start(place[:], dst)
         nc.sync.dma_start(gates[:], gate)
 
+        nc.vector.memset(zero[:], 0.0)
+        nc.vector.memset(scales[0:BASE, :].bitcast(I32), 0)
         nc.vector.memset(window[0][:], 0.0)
-        nc.scalar.activation(window[1][:], window[0][:], GELU)
+        nc.scalar.activation(window[1][:], zero[:].to_broadcast([P, U]), GELU)
 
-        nc.vector.tensor_copy(picked_scales[:], scales[:].indirect(pick[:]))
+        def move_rows(queue, h):
+            for r in range(4):
+                queue.dma_start(
+                    plane[h][r:P:32, :].bitcast(I32),
+                    picked_scales[BASE + r : P : 4, h * HALF : (h + 1) * HALF].bitcast(I32),
+                )
+
+        for a, b in ((0, HALF), (HALF, S)):
+            nc.vector.tensor_copy(picked_scales[:, a:b], scales[:].indirect(entries(pick, a, b)))
+        move_rows(nc.scalar, 0)
         nc.vector.tensor_copy(picked_words[0][:], words[:].indirect(entries(pick, 0, HALF)))
         quantise(0)
+        plane.append(keep.tile([P, HALF], U8, name="plane1", tag="w_bf0", align_bytes=64))
+        move_rows(nc.sync, 1)
         picked_words.append(keep.tile([P, HALF], U32, name="picked_words1", tag="shared", align_bytes=64))
         nc.vector.tensor_copy(picked_words[1][:], words[:].indirect(entries(pick, HALF, S)))
         quantise(1)
 
-        for blk in range(2):
-            layer(blk, 0, FIRST)
-            scatter(blk, 0, FIRST)
-        for blk in range(2):
-            for a, b in PIECES[1:]:
-                layer(blk, a, b)
-            scatter(blk, FIRST, S)
-            nc.sync.dma_start(out[blk * P : (blk + 1) * P, :], window[blk][:])
+        layer(0, 0, FIRST)
+        scatter(0, 0, FIRST)
+        layer(1, 0, HALF)
+        scatter(1, 0, HALF)
+        for a, b in PIECES[1:]:
+            layer(0, a, b)
+        scatter(0, FIRST, S)
+        nc.sync.dma_start(out[0:P, :], window[0][:])
+        layer(1, HALF, S)
+        scatter(1, HALF, S)
+        nc.sync.dma_start(out[P:N, :], window[1][:])

@@ -34,8 +34,8 @@ def tile_picked_route2_lingelu_p_kernel(tc, x_words, x_scales, gate, w1, offs, d
         pick = keep.tile([P, S // LANES], U16, name="pick")
         place = keep.tile([P, S // LANES], U16, name="place")
         words = keep.tile([P, T], U32, name="words", align_bytes=64)
-        scales = keep.tile([P, T], U8, name="scales", align_bytes=64)
-        picked_scales = keep.tile([P, S], U8, name="picked_scales", align_bytes=64)
+        scales = keep.tile([P, T], U8, name="scales", tag="table", align_bytes=64)
+        picked_scales = [keep.tile([P, HALF], U8, name="picked_scales%d" % h, align_bytes=64) for h in range(2)]
         plane = [keep.tile([P, HALF], U8, name="plane0", align_bytes=64)]
         zero = keep.tile([P, 1], F32, name="zero")
         w_raw = [
@@ -45,7 +45,7 @@ def tile_picked_route2_lingelu_p_kernel(tc, x_words, x_scales, gate, w1, offs, d
         w_bf = [keep.tile([P, P, PACK], BF16, name="w_bf%d" % b, tag="w_bf%d" % b, align_bytes=64) for b in range(2)]
         w_words = [keep.tile([P, P], U32, name="w_words%d" % b, align_bytes=64) for b in range(2)]
         w_scales = [keep.tile([P, P], U8, name="w_scales%d" % b, align_bytes=64) for b in range(2)]
-        gates = keep.tile([P, S], F32, name="gates")
+        gates = [keep.tile([P, FIRST], F32, name="gates0")]
         y = [keep.tile([P, S], F32, name="y%d" % b) for b in range(2)]
         window = [keep.tile([P, U], F32, name="window%d" % b) for b in range(2)]
         picked_words = [keep.tile([P, HALF], U32, name="picked_words0", align_bytes=64)]
@@ -80,7 +80,7 @@ def tile_picked_route2_lingelu_p_kernel(tc, x_words, x_scales, gate, w1, offs, d
 
         def scatter(blk, a, b):
             nc.vector.tensor_tensor(
-                window[blk][:].indirect(entries(place, a, b)), y[blk][:, a:b], gates[:, a:b], MULT
+                window[blk][:].indirect(entries(place, a, b)), y[blk][:, a:b], gates[a // FIRST][:], MULT
             )
 
         x_flat = x_words[0].rearrange("p n t -> p (n t)").bitcast(I32)
@@ -91,7 +91,7 @@ def tile_picked_route2_lingelu_p_kernel(tc, x_words, x_scales, gate, w1, offs, d
         for blk in range(2):
             nc.sync.dma_start(w_raw[blk][:], w_rows[:, :, blk * P : (blk + 1) * P])
         nc.sync.dma_start(place[:], dst)
-        nc.sync.dma_start(gates[:], gate)
+        nc.sync.dma_start(gates[0][:], gate[:, :FIRST])
 
         nc.vector.memset(zero[:], 0.0)
         nc.vector.memset(scales[0:BASE, :].bitcast(I32), 0)
@@ -102,12 +102,14 @@ def tile_picked_route2_lingelu_p_kernel(tc, x_words, x_scales, gate, w1, offs, d
             for r in range(4):
                 queue.dma_start(
                     plane[h][r:P:32, :].bitcast(I32),
-                    picked_scales[BASE + r : P : 4, h * HALF : (h + 1) * HALF].bitcast(I32),
+                    picked_scales[h][BASE + r : P : 4, :].bitcast(I32),
                 )
 
-        for a, b in ((0, HALF), (HALF, S)):
-            nc.vector.tensor_copy(picked_scales[:, a:b], scales[:].indirect(entries(pick, a, b)))
-        move_rows(nc.scalar, 0)
+        for h in range(2):
+            nc.vector.tensor_copy(picked_scales[h][:], scales[:].indirect(entries(pick, h * HALF, (h + 1) * HALF)))
+        move_rows(nc.sync, 0)
+        gates.append(keep.tile([P, S - FIRST], F32, name="gates1", tag="table", align_bytes=64))
+        nc.sync.dma_start(gates[1][:], gate[:, FIRST:])
         nc.vector.tensor_copy(picked_words[0][:], words[:].indirect(entries(pick, 0, HALF)))
         quantise(0)
         plane.append(keep.tile([P, HALF], U8, name="plane1", tag="w_bf0", align_bytes=64))
@@ -116,14 +118,11 @@ def tile_picked_route2_lingelu_p_kernel(tc, x_words, x_scales, gate, w1, offs, d
         nc.vector.tensor_copy(picked_words[1][:], words[:].indirect(entries(pick, HALF, S)))
         quantise(1)
 
-        layer(0, 0, FIRST)
-        scatter(0, 0, FIRST)
-        layer(1, 0, HALF)
-        scatter(1, 0, HALF)
-        for a, b in PIECES[1:]:
-            layer(0, a, b)
-        scatter(0, FIRST, S)
-        nc.sync.dma_start(out[0:P, :], window[0][:])
-        layer(1, HALF, S)
-        scatter(1, HALF, S)
-        nc.sync.dma_start(out[P:N, :], window[1][:])
+        for blk in range(2):
+            layer(blk, 0, FIRST)
+            scatter(blk, 0, FIRST)
+        for blk in range(2):
+            for a, b in PIECES[1:]:
+                layer(blk, a, b)
+            scatter(blk, FIRST, S)
+            nc.sync.dma_start(out[blk * P : (blk + 1) * P, :], window[blk][:])

@@ -45,7 +45,6 @@ def tile_picked_route2_lingelu_p_kernel(tc, x_words, x_scales, gate, w1, offs, d
         w_bf = [keep.tile([P, P, PACK], BF16, name="w_bf%d" % b, tag="w_bf%d" % b, align_bytes=64) for b in range(2)]
         w_words = [keep.tile([P, P], U32, name="w_words%d" % b, align_bytes=64) for b in range(2)]
         w_scales = [keep.tile([P, P], U8, name="w_scales%d" % b, align_bytes=64) for b in range(2)]
-        gates = [keep.tile([P, FIRST], F32, name="gates0")]
         y = [keep.tile([P, S], F32, name="y%d" % b) for b in range(2)]
         window = [keep.tile([P, U], F32, name="window%d" % b) for b in range(2)]
         picked_words = [keep.tile([P, HALF], U32, name="picked_words0", align_bytes=64)]
@@ -80,22 +79,22 @@ def tile_picked_route2_lingelu_p_kernel(tc, x_words, x_scales, gate, w1, offs, d
 
         def scatter(blk, a, b):
             nc.vector.tensor_tensor(
-                window[blk][:].indirect(entries(place, a, b)), y[blk][:, a:b], gates[a // FIRST][:], MULT
+                window[blk][:].indirect(entries(place, a, b)), y[blk][:, a:b], gates[:, a:b], MULT
             )
 
         x_flat = x_words[0].rearrange("p n t -> p (n t)").bitcast(I32)
         w_rows = w1.rearrange("(p j) m -> p j m", j=PACK)
-        nc.sync.dma_start(pick[:], offs)
         nc.sync.dma_start(scales[BASE:P, :].bitcast(I32), x_scales[0].bitcast(I32))
+        nc.sync.dma_start(pick[:], offs)
         nc.sync.dma_start(words[:].bitcast(I32), x_flat)
         for blk in range(2):
             nc.sync.dma_start(w_raw[blk][:], w_rows[:, :, blk * P : (blk + 1) * P])
         nc.sync.dma_start(place[:], dst)
-        nc.sync.dma_start(gates[0][:], gate[:, :FIRST])
 
         nc.vector.memset(zero[:], 0.0)
         nc.vector.memset(scales[0:BASE, :].bitcast(I32), 0)
-        nc.vector.memset(window[0][:], 0.0)
+        nc.vector.memset(window[0][:, : U // 2], 0.0)
+        nc.scalar.activation(window[0][:, U // 2 :], zero[:].to_broadcast([P, U // 2]), GELU)
         nc.scalar.activation(window[1][:], zero[:].to_broadcast([P, U]), GELU)
 
         def move_rows(queue, h):
@@ -108,8 +107,9 @@ def tile_picked_route2_lingelu_p_kernel(tc, x_words, x_scales, gate, w1, offs, d
         for h in range(2):
             nc.vector.tensor_copy(picked_scales[h][:], scales[:].indirect(entries(pick, h * HALF, (h + 1) * HALF)))
         move_rows(nc.sync, 0)
-        gates.append(keep.tile([P, S - FIRST], F32, name="gates1", tag="table", align_bytes=64))
-        nc.sync.dma_start(gates[1][:], gate[:, FIRST:])
+        gates = keep.tile([P, S], F32, name="gates", tag="table", align_bytes=64)
+        nc.sync.dma_start(gates[:, :FIRST], gate[:, :FIRST])
+        nc.sync.dma_start(gates[:, FIRST:], gate[:, FIRST:])
         nc.vector.tensor_copy(picked_words[0][:], words[:].indirect(entries(pick, 0, HALF)))
         quantise(0)
         plane.append(keep.tile([P, HALF], U8, name="plane1", tag="w_bf0", align_bytes=64))

@@ -22,6 +22,7 @@ ROWS = 16
 BASE = P - ROWS
 HALF = S // 2
 FIRST = 256
+CLEARED = 3 * U // 4
 PIECES = ((0, FIRST), (FIRST, HALF), (HALF, S))
 
 
@@ -38,10 +39,11 @@ def tile_picked_route2_lingelu_p_kernel(tc, x_words, x_scales, gate, w1, offs, d
         picked_scales = [keep.tile([P, HALF], U8, name="picked_scales%d" % h, align_bytes=64) for h in range(2)]
         plane = [keep.tile([P, HALF], U8, name="plane0", align_bytes=64)]
         zero = keep.tile([P, 1], F32, name="zero")
-        w_raw = [
-            keep.tile([P, PACK, P], F32, name="w_raw0", tag="shared", align_bytes=64),
-            keep.tile([P, PACK, P], F32, name="w_raw1"),
+        w_pair = [
+            keep.tile([P, 2, P], F32, name="w_pair0"),
+            keep.tile([P, 2, P], F32, name="w_pair1", tag="shared", align_bytes=64),
         ]
+        w_raw = keep.tile([P, PACK, P], F32, name="w_raw")
         w_bf = [keep.tile([P, P, PACK], BF16, name="w_bf%d" % b, tag="w_bf%d" % b, align_bytes=64) for b in range(2)]
         w_words = [keep.tile([P, P], U32, name="w_words%d" % b, align_bytes=64) for b in range(2)]
         w_scales = [keep.tile([P, P], U8, name="w_scales%d" % b, align_bytes=64) for b in range(2)]
@@ -52,11 +54,12 @@ def tile_picked_route2_lingelu_p_kernel(tc, x_words, x_scales, gate, w1, offs, d
         def entries(tile, a, b):
             return tile[:, a // LANES : b // LANES]
 
-        def quantise(blk):
+        def interleave(grouped, rows):
             nc.scalar.copy(
-                w_bf[blk][:].rearrange("p (c i) j -> p c j i", i=4),
-                w_raw[blk][:].rearrange("p j (c i) -> p c j i", i=4),
+                grouped.rearrange("p (c i) j -> p c j i", i=4), rows.rearrange("p j (c i) -> p c j i", i=4)
             )
+
+        def quantise(blk):
             nc.vector.quantize_mx(
                 out=w_words[blk][:].bitcast(FP8X4),
                 scales=w_scales[blk][:],
@@ -87,14 +90,15 @@ def tile_picked_route2_lingelu_p_kernel(tc, x_words, x_scales, gate, w1, offs, d
         nc.sync.dma_start(scales[BASE:P, :].bitcast(I32), x_scales[0].bitcast(I32))
         nc.sync.dma_start(pick[:], offs)
         nc.sync.dma_start(words[:].bitcast(I32), x_flat)
-        for blk in range(2):
-            nc.sync.dma_start(w_raw[blk][:], w_rows[:, :, blk * P : (blk + 1) * P])
+        for u in range(2):
+            nc.sync.dma_start(w_pair[u][:], w_rows[:, 2 * u : 2 * u + 2, :P])
+        nc.sync.dma_start(w_raw[:], w_rows[:, :, P:])
         nc.sync.dma_start(place[:], dst)
 
         nc.vector.memset(zero[:], 0.0)
         nc.vector.memset(scales[0:BASE, :].bitcast(I32), 0)
-        nc.vector.memset(window[0][:, : U // 2], 0.0)
-        nc.scalar.activation(window[0][:, U // 2 :], zero[:].to_broadcast([P, U // 2]), GELU)
+        nc.vector.memset(window[0][:, :CLEARED], 0.0)
+        nc.scalar.activation(window[0][:, CLEARED:], zero[:].to_broadcast([P, U - CLEARED]), GELU)
         nc.scalar.activation(window[1][:], zero[:].to_broadcast([P, U]), GELU)
 
         def move_rows(queue, h):
@@ -111,16 +115,21 @@ def tile_picked_route2_lingelu_p_kernel(tc, x_words, x_scales, gate, w1, offs, d
         nc.sync.dma_start(gates[:, :FIRST], gate[:, :FIRST])
         nc.sync.dma_start(gates[:, FIRST:], gate[:, FIRST:])
         nc.vector.tensor_copy(picked_words[0][:], words[:].indirect(entries(pick, 0, HALF)))
+        for u in range(2):
+            interleave(w_bf[0][:, :, 2 * u : 2 * u + 2], w_pair[u][:])
         quantise(0)
         plane.append(keep.tile([P, HALF], U8, name="plane1", tag="w_bf0", align_bytes=64))
         move_rows(nc.sync, 1)
         picked_words.append(keep.tile([P, HALF], U32, name="picked_words1", tag="shared", align_bytes=64))
         nc.vector.tensor_copy(picked_words[1][:], words[:].indirect(entries(pick, HALF, S)))
+        interleave(w_bf[1][:], w_raw[:])
         quantise(1)
 
-        for blk in range(2):
-            layer(blk, 0, FIRST)
-            scatter(blk, 0, FIRST)
+        layer(0, 0, P)
+        layer(0, P, FIRST)
+        scatter(0, 0, FIRST)
+        layer(1, 0, FIRST)
+        scatter(1, 0, FIRST)
         for blk in range(2):
             for a, b in PIECES[1:]:
                 layer(blk, a, b)

@@ -87,7 +87,7 @@ def tile_picked_route2_lingelu_p_kernel(tc, x_words, x_scales, gate, w1, offs, d
 
         x_flat = x_words[0].rearrange("p n t -> p (n t)").bitcast(I32)
         w_rows = w1.rearrange("(p j) m -> p j m", j=PACK)
-        nc.sync.dma_start(scales[BASE:P, :].bitcast(I32), x_scales[0].bitcast(I32))
+        nc.scalar.dma_start(scales[BASE:P, :].bitcast(I32), x_scales[0].bitcast(I32))
         nc.sync.dma_start(pick[:], offs)
         nc.sync.dma_start(words[:].bitcast(I32), x_flat)
         for u in range(2):

@@ -24,6 +24,8 @@ HALF = S // 2
 FIRST = 256
 CLEARED = 3 * U // 4
 PIECES = ((0, FIRST), (FIRST, HALF), (HALF, S))
+CUT = 576
+EDGES = (CUT, 640, 768)
 
 
 def tile_picked_route2_lingelu_p_kernel(tc, x_words, x_scales, gate, w1, offs, dst, out):
@@ -49,7 +51,7 @@ def tile_picked_route2_lingelu_p_kernel(tc, x_words, x_scales, gate, w1, offs, d
         w_scales = [keep.tile([P, P], U8, name="w_scales%d" % b, align_bytes=64) for b in range(2)]
         y = [keep.tile([P, S], F32, name="y%d" % b) for b in range(2)]
         window = [keep.tile([P, U], F32, name="window%d" % b) for b in range(2)]
-        picked_words = [keep.tile([P, HALF], U32, name="picked_words0", align_bytes=64)]
+        picked_words = [keep.tile([P, CUT], U32, name="picked_words0", align_bytes=64)]
 
         def entries(tile, a, b):
             return tile[:, a // LANES : b // LANES]
@@ -69,15 +71,18 @@ def tile_picked_route2_lingelu_p_kernel(tc, x_words, x_scales, gate, w1, offs, d
         def layer(blk, a, b):
             acc = psum.tile([P, b - a], F32, name="acc%d_%d" % (blk, a))
             h = a // HALF
-            nc.tensor.matmul_mx(
-                out=acc[:],
-                lhsT=w_words[blk][:].bitcast(FP8X4),
-                lhsT_scale=w_scales[blk][:],
-                rhs=picked_words[h][:, a - h * HALF : b - h * HALF].bitcast(FP8X4),
-                rhs_scale=plane[h][:, a - h * HALF : b - h * HALF],
-                start=True,
-                stop=True,
-            )
+            edges = [a] + [c for c in EDGES if a < c < b] + [b]
+            for lo, hi in zip(edges, edges[1:]):
+                g = lo // CUT
+                nc.tensor.matmul_mx(
+                    out=acc[:, lo - a : hi - a],
+                    lhsT=w_words[blk][:].bitcast(FP8X4),
+                    lhsT_scale=w_scales[blk][:],
+                    rhs=picked_words[g][:, lo - g * CUT : hi - g * CUT].bitcast(FP8X4),
+                    rhs_scale=plane[h][:, lo - h * HALF : hi - h * HALF],
+                    start=True,
+                    stop=True,
+                )
             nc.scalar.activation(y[blk][:, a:b], acc[:], GELU)
 
         def scatter(blk, a, b):
@@ -114,14 +119,14 @@ def tile_picked_route2_lingelu_p_kernel(tc, x_words, x_scales, gate, w1, offs, d
         gates = keep.tile([P, S], F32, name="gates", tag="table", align_bytes=64)
         nc.sync.dma_start(gates[:, :FIRST], gate[:, :FIRST])
         nc.sync.dma_start(gates[:, FIRST:], gate[:, FIRST:])
-        nc.vector.tensor_copy(picked_words[0][:], words[:].indirect(entries(pick, 0, HALF)))
+        nc.vector.tensor_copy(picked_words[0][:], words[:].indirect(entries(pick, 0, CUT)))
         for u in range(2):
             interleave(w_bf[0][:, :, 2 * u : 2 * u + 2], w_pair[u][:])
         quantise(0)
         plane.append(keep.tile([P, HALF], U8, name="plane1", tag="w_bf0", align_bytes=64))
         move_rows(nc.sync, 1)
-        picked_words.append(keep.tile([P, HALF], U32, name="picked_words1", tag="shared", align_bytes=64))
-        nc.vector.tensor_copy(picked_words[1][:], words[:].indirect(entries(pick, HALF, S)))
+        picked_words.append(keep.tile([P, S - CUT], U32, name="picked_words1", tag="shared", align_bytes=64))
+        nc.vector.tensor_copy(picked_words[1][:], words[:].indirect(entries(pick, CUT, S)))
         interleave(w_bf[1][:], w_raw[:])
         quantise(1)
 

@@ -61,11 +61,11 @@ def tile_picked_route2_lingelu_p_kernel(tc, x_words, x_scales, gate, w1, offs, d
                 grouped.rearrange("p (c i) j -> p c j i", i=4), rows.rearrange("p j (c i) -> p c j i", i=4)
             )
 
-        def quantise(blk):
+        def quantise(blk, a=0, b=P):
             nc.vector.quantize_mx(
-                out=w_words[blk][:].bitcast(FP8X4),
-                scales=w_scales[blk][:],
-                in_=w_bf[blk][:].rearrange("p m j -> p (m j)"),
+                out=w_words[blk][:, a:b].bitcast(FP8X4),
+                scales=w_scales[blk][:, a:b],
+                in_=w_bf[blk][:, a:b, :].rearrange("p m j -> p (m j)"),
             )
 
         def layer(blk, a, b):
@@ -120,9 +120,10 @@ def tile_picked_route2_lingelu_p_kernel(tc, x_words, x_scales, gate, w1, offs, d
         nc.sync.dma_start(gates[:, :FIRST], gate[:, :FIRST])
         nc.sync.dma_start(gates[:, FIRST:], gate[:, FIRST:])
         nc.vector.tensor_copy(picked_words[0][:], words[:].indirect(entries(pick, 0, CUT)))
-        for u in range(2):
-            interleave(w_bf[0][:, :, 2 * u : 2 * u + 2], w_pair[u][:])
-        quantise(0)
+        interleave(w_bf[0][:, :, 0:2], w_pair[0][:])
+        for a in (0, P // 2):
+            interleave(w_bf[0][:, a : a + P // 2, 2:4], w_pair[1][:, :, a : a + P // 2])
+            quantise(0, a, a + P // 2)
         plane.append(keep.tile([P, HALF], U8, name="plane1", tag="w_bf0", align_bytes=64))
         move_rows(nc.sync, 1)
         picked_words.append(keep.tile([P, S - CUT], U32, name="picked_words1", tag="shared", align_bytes=64))

@@ -24,8 +24,8 @@ HALF = S // 2
 FIRST = 256
 CLEARED = 3 * U // 4
 PIECES = ((0, FIRST), (FIRST, HALF), (HALF, S))
-CUT = 576
-EDGES = (CUT, 640, 768)
+CUT = 512
+EDGES = ()
 
 
 def tile_picked_route2_lingelu_p_kernel(tc, x_words, x_scales, gate, w1, offs, dst, out):

@@ -14,6 +14,7 @@ U8 = mybir.dt.uint8
 FP8X4 = mybir.dt.float8_e4m3fn_x4
 GELU = mybir.ActivationFunctionType.Gelu_apprx_tanh
 MULT = mybir.AluOpType.mult
+ADD = mybir.AluOpType.add
 
 P = 128
 PACK = 4
@@ -32,6 +33,7 @@ def tile_picked_route2_lingelu_p_kernel(tc, x_words, x_scales, gate, w1, offs, d
     nc = tc.nc
     with ExitStack() as ctx:
         keep = ctx.enter_context(tc.tile_pool(name="keep", bufs=1))
+        reuse = ctx.enter_context(tc.tile_pool(name="reuse", bufs=1))
         psum = ctx.enter_context(tc.psum_pool(name="psum", bufs=1))
 
         pick = keep.tile([P, S // LANES], U16, name="pick")
@@ -43,10 +45,10 @@ def tile_picked_route2_lingelu_p_kernel(tc, x_words, x_scales, gate, w1, offs, d
         zero = keep.tile([P, 1], F32, name="zero")
         w_pair = [
             keep.tile([P, 2, P], F32, name="w_pair0"),
-            keep.tile([P, 2, P], F32, name="w_pair1", tag="shared", align_bytes=64),
+            reuse.tile([P, 2, P], F32, name="w_pair1", offset=1536, align_bytes=64),
         ]
         w_raw = keep.tile([P, PACK, P], F32, name="w_raw")
-        w_bf = [keep.tile([P, P, PACK], BF16, name="w_bf%d" % b, tag="w_bf%d" % b, align_bytes=64) for b in range(2)]
+        w_bf = [keep.tile([P, P, PACK], BF16, name="w_bf0", tag="w_bf0", align_bytes=64)]
         w_words = [keep.tile([P, P], U32, name="w_words%d" % b, align_bytes=64) for b in range(2)]
         w_scales = [keep.tile([P, P], U8, name="w_scales%d" % b, align_bytes=64) for b in range(2)]
         y = [keep.tile([P, S], F32, name="y%d" % b) for b in range(2)]
@@ -121,13 +123,17 @@ def tile_picked_route2_lingelu_p_kernel(tc, x_words, x_scales, gate, w1, offs, d
         nc.sync.dma_start(gates[:, FIRST:], gate[:, FIRST:])
         nc.vector.tensor_copy(picked_words[0][:], words[:].indirect(entries(pick, 0, CUT)))
         interleave(w_bf[0][:, :, 0:2], w_pair[0][:])
+        interleave(w_bf[0][:, : P // 2, 2:4], w_pair[1][:, :, : P // 2])
+        nc.gpsimd.tensor_scalar(
+            w_bf[0][:, P // 2 :, 2:4], w_pair[1][:, :, P // 2 :].rearrange("p j m -> p m j"), 1.0, 0.0, MULT, ADD
+        )
         for a in (0, P // 2):
-            interleave(w_bf[0][:, a : a + P // 2, 2:4], w_pair[1][:, :, a : a + P // 2])
             quantise(0, a, a + P // 2)
         plane.append(keep.tile([P, HALF], U8, name="plane1", tag="w_bf0", align_bytes=64))
         move_rows(nc.sync, 1)
-        picked_words.append(keep.tile([P, S - CUT], U32, name="picked_words1", tag="shared", align_bytes=64))
+        picked_words.append(reuse.tile([P, S - CUT], U32, name="picked_words1", offset=0, align_bytes=64))
         nc.vector.tensor_copy(picked_words[1][:], words[:].indirect(entries(pick, CUT, S)))
+        w_bf.append(reuse.tile([P, P, PACK], BF16, name="w_bf1", offset=2048, align_bytes=64))
         interleave(w_bf[1][:], w_raw[:])
         quantise(1)
 

@@ -134,7 +134,10 @@ def tile_picked_route2_lingelu_p_kernel(tc, x_words, x_scales, gate, w1, offs, d
         picked_words.append(reuse.tile([P, S - CUT], U32, name="picked_words1", offset=0, align_bytes=64))
         nc.vector.tensor_copy(picked_words[1][:], words[:].indirect(entries(pick, CUT, S)))
         w_bf.append(reuse.tile([P, P, PACK], BF16, name="w_bf1", offset=2048, align_bytes=64))
-        interleave(w_bf[1][:], w_raw[:])
+        interleave(w_bf[1][:, : P // 2, :], w_raw[:, :, : P // 2])
+        nc.gpsimd.tensor_scalar(
+            w_bf[1][:, P // 2 :, :], w_raw[:, :, P // 2 :].rearrange("p j m -> p m j"), 1.0, 0.0, MULT, ADD
+        )
         quantise(1)
 
         layer(0, 0, P)

@@ -13,6 +13,7 @@ U16 = mybir.dt.uint16
 U8 = mybir.dt.uint8
 FP8X4 = mybir.dt.float8_e4m3fn_x4
 GELU = mybir.ActivationFunctionType.Gelu_apprx_tanh
+COPY = mybir.ActivationFunctionType.Copy
 MULT = mybir.AluOpType.mult
 ADD = mybir.AluOpType.add
 
@@ -41,7 +42,7 @@ def tile_picked_route2_lingelu_p_kernel(tc, x_words, x_scales, gate, w1, offs, d
         words = keep.tile([P, T], U32, name="words", align_bytes=64)
         scales = keep.tile([P, T], U8, name="scales", tag="table", align_bytes=64)
         picked_scales = [keep.tile([P, HALF], U8, name="picked_scales%d" % h, align_bytes=64) for h in range(2)]
-        plane = [keep.tile([P, HALF], U8, name="plane0", align_bytes=64)]
+        plane = [keep.tile([P, HALF], U8, name="plane%d" % h, align_bytes=64) for h in range(2)]
         zero = keep.tile([P, 1], F32, name="zero")
         w_pair = [
             keep.tile([P, 2, P], F32, name="w_pair0"),
@@ -52,6 +53,7 @@ def tile_picked_route2_lingelu_p_kernel(tc, x_words, x_scales, gate, w1, offs, d
         w_words = [keep.tile([P, P], U32, name="w_words%d" % b, align_bytes=64) for b in range(2)]
         w_scales = [keep.tile([P, P], U8, name="w_scales%d" % b, align_bytes=64) for b in range(2)]
         y = [keep.tile([P, S], F32, name="y%d" % b) for b in range(2)]
+        z = [keep.tile([P, S], F32, name="z%d" % b) for b in range(2)]
         window = [keep.tile([P, U], F32, name="window%d" % b) for b in range(2)]
         picked_words = [keep.tile([P, CUT], U32, name="picked_words0", align_bytes=64)]
 
@@ -87,10 +89,8 @@ def tile_picked_route2_lingelu_p_kernel(tc, x_words, x_scales, gate, w1, offs, d
                 )
             nc.scalar.activation(y[blk][:, a:b], acc[:], GELU)
 
-        def scatter(blk, a, b):
-            nc.vector.tensor_tensor(
-                window[blk][:].indirect(entries(place, a, b)), y[blk][:, a:b], gates[:, a:b], MULT
-            )
+        def weigh(blk, a, b):
+            nc.gpsimd.tensor_tensor(z[blk][:, a:b], y[blk][:, a:b], gates[:, a:b], MULT)
 
         x_flat = x_words[0].rearrange("p n t -> p (n t)").bitcast(I32)
         w_rows = w1.rearrange("(p j) m -> p j m", j=PACK)
@@ -120,6 +120,7 @@ def tile_picked_route2_lingelu_p_kernel(tc, x_words, x_scales, gate, w1, offs, d
         move_rows(nc.sync, 0)
         gates = keep.tile([P, S], F32, name="gates", tag="table", align_bytes=64)
         nc.sync.dma_start(gates[:, :FIRST], gate[:, :FIRST])
+        move_rows(nc.sync, 1)
         nc.sync.dma_start(gates[:, FIRST:], gate[:, FIRST:])
         nc.vector.tensor_copy(picked_words[0][:], words[:].indirect(entries(pick, 0, CUT)))
         interleave(w_bf[0][:, :, 0:2], w_pair[0][:])
@@ -129,8 +130,6 @@ def tile_picked_route2_lingelu_p_kernel(tc, x_words, x_scales, gate, w1, offs, d
         )
         for a in (0, P // 2):
             quantise(0, a, a + P // 2)
-        plane.append(keep.tile([P, HALF], U8, name="plane1", tag="w_bf0", align_bytes=64))
-        move_rows(nc.sync, 1)
         picked_words.append(reuse.tile([P, S - CUT], U32, name="picked_words1", offset=0, align_bytes=64))
         nc.vector.tensor_copy(picked_words[1][:], words[:].indirect(entries(pick, CUT, S)))
         w_bf.append(reuse.tile([P, P, PACK], BF16, name="w_bf1", offset=2048, align_bytes=64))
@@ -140,13 +139,14 @@ def tile_picked_route2_lingelu_p_kernel(tc, x_words, x_scales, gate, w1, offs, d
         )
         quantise(1)
 
-        layer(0, 0, P)
-        layer(0, P, FIRST)
-        scatter(0, 0, FIRST)
-        layer(1, 0, FIRST)
-        scatter(1, 0, FIRST)
-        for blk in range(2):
-            for a, b in PIECES[1:]:
-                layer(blk, a, b)
-            scatter(blk, FIRST, S)
-            nc.sync.dma_start(out[blk * P : (blk + 1) * P, :], window[blk][:])
+        QUARTER = S // 4
+        for blk, a, b in ((0, 0, P), (0, P, QUARTER), (0, QUARTER, HALF), (1, 0, QUARTER), (1, QUARTER, HALF), (0, HALF, S), (1, HALF, S)):
+            layer(blk, a, b)
+        for blk, a, b in ((0, 0, P), (0, P, QUARTER), (0, QUARTER, HALF), (1, 0, 384), (0, HALF, S), (1, 384, 768), (1, 768, S)):
+            weigh(blk, a, b)
+        for a, b in ((0, QUARTER), (QUARTER, HALF), (HALF, S)):
+            nc.vector.tensor_copy(window[0][:].indirect(entries(place, a, b)), z[0][:, a:b])
+        nc.sync.dma_start(out[:P, :], window[0][:])
+        for a, b in ((0, 384), (384, 768), (768, S)):
+            nc.scalar.activation(window[1][:].indirect(entries(place, a, b)), z[1][:, a:b], COPY)
+        nc.sync.dma_start(out[P:, :], window[1][:])

@@ -24,17 +24,15 @@ ROWS = 16
 BASE = P - ROWS
 HALF = S // 2
 FIRST = 256
+PIECE = 384
+CUT = 640
 CLEARED = 3 * U // 4
-PIECES = ((0, FIRST), (FIRST, HALF), (HALF, S))
-CUT = 512
-EDGES = ()
 
 
 def tile_picked_route2_lingelu_p_kernel(tc, x_words, x_scales, gate, w1, offs, dst, out):
     nc = tc.nc
     with ExitStack() as ctx:
         keep = ctx.enter_context(tc.tile_pool(name="keep", bufs=1))
-        reuse = ctx.enter_context(tc.tile_pool(name="reuse", bufs=1))
         psum = ctx.enter_context(tc.psum_pool(name="psum", bufs=1))
 
         pick = keep.tile([P, S // LANES], U16, name="pick")
@@ -42,40 +40,49 @@ def tile_picked_route2_lingelu_p_kernel(tc, x_words, x_scales, gate, w1, offs, d
         words = keep.tile([P, T], U32, name="words", align_bytes=64)
         scales = keep.tile([P, T], U8, name="scales", tag="table", align_bytes=64)
         picked_scales = [keep.tile([P, HALF], U8, name="picked_scales%d" % h, align_bytes=64) for h in range(2)]
-        plane = [keep.tile([P, HALF], U8, name="plane%d" % h, align_bytes=64) for h in range(2)]
+        plane = keep.tile([P, S], U8, name="plane", align_bytes=64)
         zero = keep.tile([P, 1], F32, name="zero")
-        w_pair = [
-            keep.tile([P, 2, P], F32, name="w_pair0"),
-            reuse.tile([P, 2, P], F32, name="w_pair1", offset=1536, align_bytes=64),
+        w_raw = keep.tile([P, PACK, N], F32, name="w_raw", tag="raw", align_bytes=64)
+        w_bf = [keep.tile([P, P, PACK], BF16, name="w_bf%d" % b, align_bytes=64) for b in range(2)]
+        w_words = [
+            keep.tile([P, P], U32, name="w_words0", tag="stationary0", align_bytes=64),
+            keep.tile([P, P], U32, name="w_words1", align_bytes=64),
         ]
-        w_raw = keep.tile([P, PACK, P], F32, name="w_raw")
-        w_bf = [keep.tile([P, P, PACK], BF16, name="w_bf0", tag="w_bf0", align_bytes=64)]
-        w_words = [keep.tile([P, P], U32, name="w_words%d" % b, align_bytes=64) for b in range(2)]
         w_scales = [keep.tile([P, P], U8, name="w_scales%d" % b, align_bytes=64) for b in range(2)]
         y = [keep.tile([P, S], F32, name="y%d" % b) for b in range(2)]
-        z = [keep.tile([P, S], F32, name="z%d" % b) for b in range(2)]
         window = [keep.tile([P, U], F32, name="window%d" % b) for b in range(2)]
         picked_words = [keep.tile([P, CUT], U32, name="picked_words0", align_bytes=64)]
 
         def entries(tile, a, b):
             return tile[:, a // LANES : b // LANES]
 
-        def interleave(grouped, rows):
+        def round_weights(blk):
+            raw = w_raw[:, :, blk * P : (blk + 1) * P]
             nc.scalar.copy(
-                grouped.rearrange("p (c i) j -> p c j i", i=4), rows.rearrange("p j (c i) -> p c j i", i=4)
+                w_bf[blk][:, : P // 2, :].rearrange("p (c i) j -> p c j i", i=4),
+                raw[:, :, : P // 2].rearrange("p j (c i) -> p c j i", i=4),
+            )
+            nc.gpsimd.tensor_scalar(
+                w_bf[blk][:, P // 2 :, :], raw[:, :, P // 2 :].rearrange("p j m -> p m j"), 1.0, 0.0, MULT, ADD
             )
 
-        def quantise(blk, a=0, b=P):
+        def quantise(blk):
             nc.vector.quantize_mx(
-                out=w_words[blk][:, a:b].bitcast(FP8X4),
-                scales=w_scales[blk][:, a:b],
-                in_=w_bf[blk][:, a:b, :].rearrange("p m j -> p (m j)"),
+                out=w_words[blk][:].bitcast(FP8X4),
+                scales=w_scales[blk][:],
+                in_=w_bf[blk][:].rearrange("p m j -> p (m j)"),
             )
 
-        def layer(blk, a, b):
+        def move_rows(h):
+            for r in range(4):
+                nc.sync.dma_start(
+                    plane[r:P:32, h * HALF : (h + 1) * HALF].bitcast(I32),
+                    picked_scales[h][BASE + r : P : 4, :].bitcast(I32),
+                )
+
+        def layer(blk, edges):
+            a, b = edges[0], edges[-1]
             acc = psum.tile([P, b - a], F32, name="acc%d_%d" % (blk, a))
-            h = a // HALF
-            edges = [a] + [c for c in EDGES if a < c < b] + [b]
             for lo, hi in zip(edges, edges[1:]):
                 g = lo // CUT
                 nc.tensor.matmul_mx(
@@ -83,23 +90,21 @@ def tile_picked_route2_lingelu_p_kernel(tc, x_words, x_scales, gate, w1, offs, d
                     lhsT=w_words[blk][:].bitcast(FP8X4),
                     lhsT_scale=w_scales[blk][:],
                     rhs=picked_words[g][:, lo - g * CUT : hi - g * CUT].bitcast(FP8X4),
-                    rhs_scale=plane[h][:, lo - h * HALF : hi - h * HALF],
+                    rhs_scale=plane[:, lo:hi],
                     start=True,
                     stop=True,
                 )
             nc.scalar.activation(y[blk][:, a:b], acc[:], GELU)
 
-        def weigh(blk, a, b):
-            nc.gpsimd.tensor_tensor(z[blk][:, a:b], y[blk][:, a:b], gates[:, a:b], MULT)
+        def weigh_and_scatter(blk, a, b):
+            nc.vector.tensor_tensor(
+                window[blk][:].indirect(entries(place, a, b)), y[blk][:, a:b], gates[:, a:b], MULT
+            )
 
-        x_flat = x_words[0].rearrange("p n t -> p (n t)").bitcast(I32)
-        w_rows = w1.rearrange("(p j) m -> p j m", j=PACK)
         nc.scalar.dma_start(scales[BASE:P, :].bitcast(I32), x_scales[0].bitcast(I32))
         nc.sync.dma_start(pick[:], offs)
-        nc.sync.dma_start(words[:].bitcast(I32), x_flat)
-        for u in range(2):
-            nc.sync.dma_start(w_pair[u][:], w_rows[:, 2 * u : 2 * u + 2, :P])
-        nc.sync.dma_start(w_raw[:], w_rows[:, :, P:])
+        nc.sync.dma_start(words[:].bitcast(I32), x_words[0].rearrange("p n t -> p (n t)").bitcast(I32))
+        nc.sync.dma_start(w_raw[:], w1.rearrange("(p j) m -> p j m", j=PACK))
         nc.sync.dma_start(place[:], dst)
 
         nc.vector.memset(zero[:], 0.0)
@@ -108,45 +113,29 @@ def tile_picked_route2_lingelu_p_kernel(tc, x_words, x_scales, gate, w1, offs, d
         nc.scalar.activation(window[0][:, CLEARED:], zero[:].to_broadcast([P, U - CLEARED]), GELU)
         nc.scalar.activation(window[1][:], zero[:].to_broadcast([P, U]), GELU)
 
-        def move_rows(queue, h):
-            for r in range(4):
-                queue.dma_start(
-                    plane[h][r:P:32, :].bitcast(I32),
-                    picked_scales[h][BASE + r : P : 4, :].bitcast(I32),
-                )
-
         for h in range(2):
             nc.vector.tensor_copy(picked_scales[h][:], scales[:].indirect(entries(pick, h * HALF, (h + 1) * HALF)))
-        move_rows(nc.sync, 0)
+        move_rows(0)
         gates = keep.tile([P, S], F32, name="gates", tag="table", align_bytes=64)
-        nc.sync.dma_start(gates[:, :FIRST], gate[:, :FIRST])
-        move_rows(nc.sync, 1)
-        nc.sync.dma_start(gates[:, FIRST:], gate[:, FIRST:])
+        nc.sync.dma_start(gates[:, :PIECE], gate[:, :PIECE])
+        move_rows(1)
+        nc.sync.dma_start(gates[:, PIECE:], gate[:, PIECE:])
         nc.vector.tensor_copy(picked_words[0][:], words[:].indirect(entries(pick, 0, CUT)))
-        interleave(w_bf[0][:, :, 0:2], w_pair[0][:])
-        interleave(w_bf[0][:, : P // 2, 2:4], w_pair[1][:, :, : P // 2])
-        nc.gpsimd.tensor_scalar(
-            w_bf[0][:, P // 2 :, 2:4], w_pair[1][:, :, P // 2 :].rearrange("p j m -> p m j"), 1.0, 0.0, MULT, ADD
-        )
-        for a in (0, P // 2):
-            quantise(0, a, a + P // 2)
-        picked_words.append(reuse.tile([P, S - CUT], U32, name="picked_words1", offset=0, align_bytes=64))
+        for blk in range(2):
+            round_weights(blk)
+            quantise(blk)
+        picked_words.append(keep.tile([P, S - CUT], U32, name="picked_words1", tag="raw", align_bytes=64))
         nc.vector.tensor_copy(picked_words[1][:], words[:].indirect(entries(pick, CUT, S)))
-        w_bf.append(reuse.tile([P, P, PACK], BF16, name="w_bf1", offset=2048, align_bytes=64))
-        interleave(w_bf[1][:, : P // 2, :], w_raw[:, :, : P // 2])
-        nc.gpsimd.tensor_scalar(
-            w_bf[1][:, P // 2 :, :], w_raw[:, :, P // 2 :].rearrange("p j m -> p m j"), 1.0, 0.0, MULT, ADD
-        )
-        quantise(1)
 
-        QUARTER = S // 4
-        for blk, a, b in ((0, 0, P), (0, P, QUARTER), (0, QUARTER, HALF), (1, 0, QUARTER), (1, QUARTER, HALF), (0, HALF, S), (1, HALF, S)):
-            layer(blk, a, b)
-        for blk, a, b in ((0, 0, P), (0, P, QUARTER), (0, QUARTER, HALF), (1, 0, 384), (0, HALF, S), (1, 384, 768), (1, 768, S)):
-            weigh(blk, a, b)
-        for a, b in ((0, QUARTER), (QUARTER, HALF), (HALF, S)):
-            nc.vector.tensor_copy(window[0][:].indirect(entries(place, a, b)), z[0][:, a:b])
+        for blk, edges in ((0, (0, 256)), (1, (0, 256, 384)), (0, (256, 512, 640)), (1, (384, 512, 640, 768)), (0, (640, 896, S)), (1, (768, S))):
+            layer(blk, edges)
+        weighted = keep.tile([P, 2 * PIECE], F32, name="weighted", tag="stationary0", align_bytes=64)
+        weigh_and_scatter(0, 0, FIRST)
+        for a in (0, PIECE):
+            nc.vector.tensor_tensor(weighted[:, a : a + PIECE], y[1][:, a : a + PIECE], gates[:, a : a + PIECE], MULT)
+        weigh_and_scatter(0, FIRST, S)
         nc.sync.dma_start(out[:P, :], window[0][:])
-        for a, b in ((0, 384), (384, 768), (768, S)):
-            nc.scalar.activation(window[1][:].indirect(entries(place, a, b)), z[1][:, a:b], COPY)
+        for a in (0, PIECE):
+            nc.scalar.activation(window[1][:].indirect(entries(place, a, a + PIECE)), weighted[:, a : a + PIECE], COPY)
+        weigh_and_scatter(1, 2 * PIECE, S)
         nc.sync.dma_start(out[P:, :], window[1][:])

@@ -22,11 +22,13 @@ PACK = 4
 LANES = 16
 ROWS = 16
 BASE = P - ROWS
+CLEARED = 3 * U // 4
 HALF = S // 2
 FIRST = 256
 PIECE = 384
 CUT = 640
-CLEARED = 3 * U // 4
+LAST = 672
+SHARES = ((0, PIECE), (PIECE, LAST))
 
 
 def tile_picked_route2_lingelu_p_kernel(tc, x_words, x_scales, gate, w1, offs, dst, out):
@@ -35,36 +37,31 @@ def tile_picked_route2_lingelu_p_kernel(tc, x_words, x_scales, gate, w1, offs, d
         keep = ctx.enter_context(tc.tile_pool(name="keep", bufs=1))
         psum = ctx.enter_context(tc.psum_pool(name="psum", bufs=1))
 
+        def tile(shape, dtype, name, tag=None):
+            return keep.tile([P] + shape, dtype, name=name, tag=tag or name, align_bytes=64)
+
         pick = keep.tile([P, S // LANES], U16, name="pick")
         place = keep.tile([P, S // LANES], U16, name="place")
-        words = keep.tile([P, T], U32, name="words", align_bytes=64)
-        scales = keep.tile([P, T], U8, name="scales", tag="table", align_bytes=64)
-        picked_scales = [keep.tile([P, HALF], U8, name="picked_scales%d" % h, align_bytes=64) for h in range(2)]
-        plane = keep.tile([P, S], U8, name="plane", align_bytes=64)
-        zero = keep.tile([P, 1], F32, name="zero")
-        w_raw = keep.tile([P, PACK, N], F32, name="w_raw", tag="raw", align_bytes=64)
-        w_bf = [keep.tile([P, P, PACK], BF16, name="w_bf%d" % b, align_bytes=64) for b in range(2)]
-        w_words = [
-            keep.tile([P, P], U32, name="w_words0", tag="stationary0", align_bytes=64),
-            keep.tile([P, P], U32, name="w_words1", align_bytes=64),
-        ]
-        w_scales = [keep.tile([P, P], U8, name="w_scales%d" % b, align_bytes=64) for b in range(2)]
-        y = [keep.tile([P, S], F32, name="y%d" % b) for b in range(2)]
-        window = [keep.tile([P, U], F32, name="window%d" % b) for b in range(2)]
-        picked_words = [keep.tile([P, CUT], U32, name="picked_words0", align_bytes=64)]
+        words = tile([T], U32, "words")
+        scales = tile([T], U8, "scales", "table")
+        plane = tile([S], U8, "plane")
+        zero = tile([1], F32, "zero")
+        w_bf = [tile([P, PACK], BF16, "w_bf%d" % b) for b in range(2)]
+        w_words = [tile([P], U32, "w_words%d" % b) for b in range(2)]
+        w_scales = [tile([P], U8, "w_scales%d" % b) for b in range(2)]
+        y = [tile([S], F32, "y%d" % b) for b in range(2)]
+        window = [tile([U], F32, "window%d" % b) for b in range(2)]
+        picked_words = []
 
-        def entries(tile, a, b):
-            return tile[:, a // LANES : b // LANES]
+        def entries(offsets, a, b):
+            return offsets[:, a // LANES : b // LANES]
 
-        def round_weights(blk):
-            raw = w_raw[:, :, blk * P : (blk + 1) * P]
+        def round_weights(blk, raw, cut=P // 2):
             nc.scalar.copy(
-                w_bf[blk][:, : P // 2, :].rearrange("p (c i) j -> p c j i", i=4),
-                raw[:, :, : P // 2].rearrange("p j (c i) -> p c j i", i=4),
+                w_bf[blk][:, :cut, :].rearrange("p (c i) j -> p c j i", i=4),
+                raw[:, :, :cut].rearrange("p j (c i) -> p c j i", i=4),
             )
-            nc.gpsimd.tensor_scalar(
-                w_bf[blk][:, P // 2 :, :], raw[:, :, P // 2 :].rearrange("p j m -> p m j"), 1.0, 0.0, MULT, ADD
-            )
+            nc.gpsimd.tensor_scalar(w_bf[blk][:, cut:, :], raw[:, :, cut:].rearrange("p j m -> p m j"), 1.0, 0.0, MULT, ADD)
 
         def quantise(blk):
             nc.vector.quantize_mx(
@@ -73,23 +70,30 @@ def tile_picked_route2_lingelu_p_kernel(tc, x_words, x_scales, gate, w1, offs, d
                 in_=w_bf[blk][:].rearrange("p m j -> p (m j)"),
             )
 
-        def move_rows(h):
-            for r in range(4):
-                nc.sync.dma_start(
-                    plane[r:P:32, h * HALF : (h + 1) * HALF].bitcast(I32),
-                    picked_scales[h][BASE + r : P : 4, :].bitcast(I32),
-                )
+        def gather_scales(a, b):
+            picked = tile([b - a], U8, "picked_scales%d" % a)
+            nc.vector.tensor_copy(picked[:], scales[:].indirect(entries(pick, a, b)))
+            return picked
 
-        def layer(blk, edges):
+        def move_rows(picked, a, b):
+            for r in range(4):
+                nc.sync.dma_start(plane[r:P:32, a:b].bitcast(I32), picked[BASE + r : P : 4, :].bitcast(I32))
+
+        def gather_words(a, b, tag=None):
+            picked = tile([b - a], U32, "picked_words%d" % a, tag)
+            picked_words.append((a, b, picked))
+            nc.vector.tensor_copy(picked[:], words[:].indirect(entries(pick, a, b)))
+
+        def layer(blk, *edges):
             a, b = edges[0], edges[-1]
             acc = psum.tile([P, b - a], F32, name="acc%d_%d" % (blk, a))
             for lo, hi in zip(edges, edges[1:]):
-                g = lo // CUT
+                first, picked = [(s, t) for s, e, t in picked_words if s <= lo and hi <= e][0]
                 nc.tensor.matmul_mx(
                     out=acc[:, lo - a : hi - a],
                     lhsT=w_words[blk][:].bitcast(FP8X4),
                     lhsT_scale=w_scales[blk][:],
-                    rhs=picked_words[g][:, lo - g * CUT : hi - g * CUT].bitcast(FP8X4),
+                    rhs=picked[:, lo - first : hi - first].bitcast(FP8X4),
                     rhs_scale=plane[:, lo:hi],
                     start=True,
                     stop=True,
@@ -97,45 +101,47 @@ def tile_picked_route2_lingelu_p_kernel(tc, x_words, x_scales, gate, w1, offs, d
             nc.scalar.activation(y[blk][:, a:b], acc[:], GELU)
 
         def weigh_and_scatter(blk, a, b):
-            nc.vector.tensor_tensor(
-                window[blk][:].indirect(entries(place, a, b)), y[blk][:, a:b], gates[:, a:b], MULT
-            )
+            nc.vector.tensor_tensor(window[blk][:].indirect(entries(place, a, b)), y[blk][:, a:b], gates[:, a:b], MULT)
 
+        def clear_on_scalar(columns):
+            nc.scalar.activation(columns, zero[:].to_broadcast(list(columns.shape)), GELU)
+
+        w_rows = w1.rearrange("(p j) m -> p j m", j=PACK)
+        x_flat = x_words[0].rearrange("p n t -> p (n t)").bitcast(I32)
+        w_raw = tile([PACK, N], F32, "w_raw")
         nc.scalar.dma_start(scales[BASE:P, :].bitcast(I32), x_scales[0].bitcast(I32))
         nc.sync.dma_start(pick[:], offs)
-        nc.sync.dma_start(words[:].bitcast(I32), x_words[0].rearrange("p n t -> p (n t)").bitcast(I32))
-        nc.sync.dma_start(w_raw[:], w1.rearrange("(p j) m -> p j m", j=PACK))
+        nc.sync.dma_start(words[:].bitcast(I32), x_flat)
+        nc.sync.dma_start(w_raw[:], w_rows)
         nc.sync.dma_start(place[:], dst)
 
         nc.vector.memset(zero[:], 0.0)
         nc.vector.memset(scales[0:BASE, :].bitcast(I32), 0)
         nc.vector.memset(window[0][:, :CLEARED], 0.0)
-        nc.scalar.activation(window[0][:, CLEARED:], zero[:].to_broadcast([P, U - CLEARED]), GELU)
-        nc.scalar.activation(window[1][:], zero[:].to_broadcast([P, U]), GELU)
+        clear_on_scalar(window[0][:, CLEARED:])
+        clear_on_scalar(window[1][:])
 
-        for h in range(2):
-            nc.vector.tensor_copy(picked_scales[h][:], scales[:].indirect(entries(pick, h * HALF, (h + 1) * HALF)))
-        move_rows(0)
-        gates = keep.tile([P, S], F32, name="gates", tag="table", align_bytes=64)
+        picked_scales = [gather_scales(0, HALF), gather_scales(HALF, S)]
+        move_rows(picked_scales[0], 0, HALF)
+        gates = tile([S], F32, "gates", "table")
         nc.sync.dma_start(gates[:, :PIECE], gate[:, :PIECE])
-        move_rows(1)
+        move_rows(picked_scales[1], HALF, S)
         nc.sync.dma_start(gates[:, PIECE:], gate[:, PIECE:])
-        nc.vector.tensor_copy(picked_words[0][:], words[:].indirect(entries(pick, 0, CUT)))
+        gather_words(0, CUT)
         for blk in range(2):
-            round_weights(blk)
+            round_weights(blk, w_raw[:, :, blk * P : (blk + 1) * P], P // 2)
             quantise(blk)
-        picked_words.append(keep.tile([P, S - CUT], U32, name="picked_words1", tag="raw", align_bytes=64))
-        nc.vector.tensor_copy(picked_words[1][:], words[:].indirect(entries(pick, CUT, S)))
+        gather_words(CUT, S, "w_raw")
 
-        for blk, edges in ((0, (0, 256)), (1, (0, 256, 384)), (0, (256, 512, 640)), (1, (384, 512, 640, 768)), (0, (640, 896, S)), (1, (768, S))):
-            layer(blk, edges)
-        weighted = keep.tile([P, 2 * PIECE], F32, name="weighted", tag="stationary0", align_bytes=64)
+        for step in ((0, 0, 256), (1, 0, 256, 384), (0, 256, 512, 640), (1, 384, 512, 640, 768), (0, 640, 896, S), (1, 768, S)):
+            layer(*step)
+        weighted = tile([LAST], F32, "weighted", "w_words0")
         weigh_and_scatter(0, 0, FIRST)
-        for a in (0, PIECE):
-            nc.vector.tensor_tensor(weighted[:, a : a + PIECE], y[1][:, a : a + PIECE], gates[:, a : a + PIECE], MULT)
+        for a, b in SHARES:
+            nc.vector.tensor_tensor(weighted[:, a:b], y[1][:, a:b], gates[:, a:b], MULT)
         weigh_and_scatter(0, FIRST, S)
         nc.sync.dma_start(out[:P, :], window[0][:])
-        for a in (0, PIECE):
-            nc.scalar.activation(window[1][:].indirect(entries(place, a, a + PIECE)), weighted[:, a : a + PIECE], COPY)
-        weigh_and_scatter(1, 2 * PIECE, S)
+        for a, b in SHARES:
+            nc.scalar.activation(window[1][:].indirect(entries(place, a, b)), weighted[:, a:b], COPY)
+        weigh_and_scatter(1, LAST, S)
         nc.sync.dma_start(out[P:, :], window[1][:])

@@ -22,126 +22,135 @@ PACK = 4
 LANES = 16
 ROWS = 16
 BASE = P - ROWS
-CLEARED = 3 * U // 4
 HALF = S // 2
-FIRST = 256
-PIECE = 384
-CUT = 640
+FIRST = 384
+CLEARED = 3 * U // 4
+CUT = 512
+EDGES = (256, 512)
 LAST = 672
-SHARES = ((0, PIECE), (PIECE, LAST))
+SHARES = ((0, 384), (384, LAST))
 
 
 def tile_picked_route2_lingelu_p_kernel(tc, x_words, x_scales, gate, w1, offs, dst, out):
     nc = tc.nc
     with ExitStack() as ctx:
         keep = ctx.enter_context(tc.tile_pool(name="keep", bufs=1))
+        reuse = ctx.enter_context(tc.tile_pool(name="reuse", bufs=1))
         psum = ctx.enter_context(tc.psum_pool(name="psum", bufs=1))
-
-        def tile(shape, dtype, name, tag=None):
-            return keep.tile([P] + shape, dtype, name=name, tag=tag or name, align_bytes=64)
 
         pick = keep.tile([P, S // LANES], U16, name="pick")
         place = keep.tile([P, S // LANES], U16, name="place")
-        words = tile([T], U32, "words")
-        scales = tile([T], U8, "scales", "table")
-        plane = tile([S], U8, "plane")
-        zero = tile([1], F32, "zero")
-        w_bf = [tile([P, PACK], BF16, "w_bf%d" % b) for b in range(2)]
-        w_words = [tile([P], U32, "w_words%d" % b) for b in range(2)]
-        w_scales = [tile([P], U8, "w_scales%d" % b) for b in range(2)]
-        y = [tile([S], F32, "y%d" % b) for b in range(2)]
-        window = [tile([U], F32, "window%d" % b) for b in range(2)]
-        picked_words = []
+        words = keep.tile([P, T], U32, name="words", align_bytes=64)
+        scales = keep.tile([P, T], U8, name="scales", tag="table", align_bytes=64)
+        picked_scales = [keep.tile([P, HALF], U8, name="picked_scales%d" % h, align_bytes=64) for h in range(2)]
+        plane = [keep.tile([P, HALF], U8, name="plane%d" % h, align_bytes=64) for h in range(2)]
+        zero = keep.tile([P, 1], F32, name="zero")
+        w_pair = [
+            keep.tile([P, 2, P], F32, name="w_pair0"),
+            reuse.tile([P, 2, P], F32, name="w_pair1", offset=1536, align_bytes=64),
+        ]
+        w_raw = reuse.tile([P, PACK, P], F32, name="w_raw", offset=4096, align_bytes=64)
+        w_bf = [keep.tile([P, P, PACK], BF16, name="w_bf0", tag="w_bf0", align_bytes=64)]
+        w_words = [
+            reuse.tile([P, P], U32, name="w_words0", offset=8192, align_bytes=64),
+            keep.tile([P, P], U32, name="w_words1", align_bytes=64),
+        ]
+        w_scales = [keep.tile([P, P], U8, name="w_scales%d" % b, align_bytes=64) for b in range(2)]
+        y = [keep.tile([P, S], F32, name="y%d" % b) for b in range(2)]
+        window = [keep.tile([P, U], F32, name="window%d" % b) for b in range(2)]
+        picked_words = [keep.tile([P, CUT], U32, name="picked_words0", align_bytes=64)]
 
-        def entries(offsets, a, b):
-            return offsets[:, a // LANES : b // LANES]
+        def entries(tile, a, b):
+            return tile[:, a // LANES : b // LANES]
 
-        def round_weights(blk, raw, cut=P // 2):
+        def interleave(grouped, rows):
             nc.scalar.copy(
-                w_bf[blk][:, :cut, :].rearrange("p (c i) j -> p c j i", i=4),
-                raw[:, :, :cut].rearrange("p j (c i) -> p c j i", i=4),
+                grouped.rearrange("p (c i) j -> p c j i", i=4), rows.rearrange("p j (c i) -> p c j i", i=4)
             )
-            nc.gpsimd.tensor_scalar(w_bf[blk][:, cut:, :], raw[:, :, cut:].rearrange("p j m -> p m j"), 1.0, 0.0, MULT, ADD)
 
-        def quantise(blk):
+        def quantise(blk, a=0, b=P):
             nc.vector.quantize_mx(
-                out=w_words[blk][:].bitcast(FP8X4),
-                scales=w_scales[blk][:],
-                in_=w_bf[blk][:].rearrange("p m j -> p (m j)"),
+                out=w_words[blk][:, a:b].bitcast(FP8X4),
+                scales=w_scales[blk][:, a:b],
+                in_=w_bf[blk][:, a:b, :].rearrange("p m j -> p (m j)"),
             )
 
-        def gather_scales(a, b):
-            picked = tile([b - a], U8, "picked_scales%d" % a)
-            nc.vector.tensor_copy(picked[:], scales[:].indirect(entries(pick, a, b)))
-            return picked
-
-        def move_rows(picked, a, b):
-            for r in range(4):
-                nc.sync.dma_start(plane[r:P:32, a:b].bitcast(I32), picked[BASE + r : P : 4, :].bitcast(I32))
-
-        def gather_words(a, b, tag=None):
-            picked = tile([b - a], U32, "picked_words%d" % a, tag)
-            picked_words.append((a, b, picked))
-            nc.vector.tensor_copy(picked[:], words[:].indirect(entries(pick, a, b)))
-
-        def layer(blk, *edges):
-            a, b = edges[0], edges[-1]
+        def layer(blk, a, b):
             acc = psum.tile([P, b - a], F32, name="acc%d_%d" % (blk, a))
+            edges = [a] + [c for c in EDGES if a < c < b] + [b]
             for lo, hi in zip(edges, edges[1:]):
-                first, picked = [(s, t) for s, e, t in picked_words if s <= lo and hi <= e][0]
+                g = lo // CUT
+                h = lo // HALF
                 nc.tensor.matmul_mx(
                     out=acc[:, lo - a : hi - a],
                     lhsT=w_words[blk][:].bitcast(FP8X4),
                     lhsT_scale=w_scales[blk][:],
-                    rhs=picked[:, lo - first : hi - first].bitcast(FP8X4),
-                    rhs_scale=plane[:, lo:hi],
+                    rhs=picked_words[g][:, lo - g * CUT : hi - g * CUT].bitcast(FP8X4),
+                    rhs_scale=plane[h][:, lo - h * HALF : hi - h * HALF],
                     start=True,
                     stop=True,
                 )
             nc.scalar.activation(y[blk][:, a:b], acc[:], GELU)
 
-        def weigh_and_scatter(blk, a, b):
+        def scatter(blk, a, b):
             nc.vector.tensor_tensor(window[blk][:].indirect(entries(place, a, b)), y[blk][:, a:b], gates[:, a:b], MULT)
 
-        def clear_on_scalar(columns):
-            nc.scalar.activation(columns, zero[:].to_broadcast(list(columns.shape)), GELU)
-
-        w_rows = w1.rearrange("(p j) m -> p j m", j=PACK)
         x_flat = x_words[0].rearrange("p n t -> p (n t)").bitcast(I32)
-        w_raw = tile([PACK, N], F32, "w_raw")
+        w_rows = w1.rearrange("(p j) m -> p j m", j=PACK)
         nc.scalar.dma_start(scales[BASE:P, :].bitcast(I32), x_scales[0].bitcast(I32))
         nc.sync.dma_start(pick[:], offs)
         nc.sync.dma_start(words[:].bitcast(I32), x_flat)
-        nc.sync.dma_start(w_raw[:], w_rows)
+        for u in range(2):
+            nc.sync.dma_start(w_pair[u][:], w_rows[:, 2 * u : 2 * u + 2, :P])
+        nc.sync.dma_start(w_raw[:], w_rows[:, :, P:])
         nc.sync.dma_start(place[:], dst)
 
         nc.vector.memset(zero[:], 0.0)
         nc.vector.memset(scales[0:BASE, :].bitcast(I32), 0)
         nc.vector.memset(window[0][:, :CLEARED], 0.0)
-        clear_on_scalar(window[0][:, CLEARED:])
-        clear_on_scalar(window[1][:])
+        nc.scalar.activation(window[0][:, CLEARED:], zero[:].to_broadcast([P, U - CLEARED]), GELU)
+        nc.scalar.activation(window[1][:], zero[:].to_broadcast([P, U]), GELU)
 
-        picked_scales = [gather_scales(0, HALF), gather_scales(HALF, S)]
-        move_rows(picked_scales[0], 0, HALF)
-        gates = tile([S], F32, "gates", "table")
-        nc.sync.dma_start(gates[:, :PIECE], gate[:, :PIECE])
-        move_rows(picked_scales[1], HALF, S)
-        nc.sync.dma_start(gates[:, PIECE:], gate[:, PIECE:])
-        gather_words(0, CUT)
-        for blk in range(2):
-            round_weights(blk, w_raw[:, :, blk * P : (blk + 1) * P], P // 2)
-            quantise(blk)
-        gather_words(CUT, S, "w_raw")
+        def move_rows(queue, h):
+            for r in range(4):
+                queue.dma_start(
+                    plane[h][r:P:32, :].bitcast(I32),
+                    picked_scales[h][BASE + r : P : 4, :].bitcast(I32),
+                )
 
-        for step in ((0, 0, 256), (1, 0, 256, 384), (0, 256, 512, 640), (1, 384, 512, 640, 768), (0, 640, 896, S), (1, 768, S)):
-            layer(*step)
-        weighted = tile([LAST], F32, "weighted", "w_words0")
-        weigh_and_scatter(0, 0, FIRST)
+        for h in range(2):
+            nc.vector.tensor_copy(picked_scales[h][:], scales[:].indirect(entries(pick, h * HALF, (h + 1) * HALF)))
+        move_rows(nc.sync, 0)
+        gates = keep.tile([P, S], F32, name="gates", tag="table", align_bytes=64)
+        nc.sync.dma_start(gates[:, :FIRST], gate[:, :FIRST])
+        move_rows(nc.sync, 1)
+        nc.sync.dma_start(gates[:, FIRST:], gate[:, FIRST:])
+        nc.vector.tensor_copy(picked_words[0][:], words[:].indirect(entries(pick, 0, CUT)))
+        interleave(w_bf[0][:, :, 0:2], w_pair[0][:])
+        interleave(w_bf[0][:, : P // 2, 2:4], w_pair[1][:, :, : P // 2])
+        nc.gpsimd.tensor_scalar(
+            w_bf[0][:, P // 2 :, 2:4], w_pair[1][:, :, P // 2 :].rearrange("p j m -> p m j"), 1.0, 0.0, MULT, ADD
+        )
+        for a in (0, P // 2):
+            quantise(0, a, a + P // 2)
+        picked_words.append(reuse.tile([P, S - CUT], U32, name="picked_words1", offset=4096, align_bytes=64))
+        w_bf.append(reuse.tile([P, P, PACK], BF16, name="w_bf1", offset=2048, align_bytes=64))
+        interleave(w_bf[1][:, : P // 2, :], w_raw[:, :, : P // 2])
+        nc.gpsimd.tensor_scalar(
+            w_bf[1][:, P // 2 :, :], w_raw[:, :, P // 2 :].rearrange("p j m -> p m j"), 1.0, 0.0, MULT, ADD
+        )
+        quantise(1)
+        nc.vector.tensor_copy(picked_words[1][:], words[:].indirect(entries(pick, CUT, S)))
+
+        for blk, a, b in ((0, 0, 256), (1, 0, 384), (0, 256, HALF), (1, 384, 768), (0, HALF, S), (1, 768, S)):
+            layer(blk, a, b)
+        weighted = reuse.tile([P, LAST], F32, name="weighted", offset=8192, align_bytes=64)
+        scatter(0, 0, 256)
         for a, b in SHARES:
             nc.vector.tensor_tensor(weighted[:, a:b], y[1][:, a:b], gates[:, a:b], MULT)
-        weigh_and_scatter(0, FIRST, S)
+        scatter(0, 256, S)
         nc.sync.dma_start(out[:P, :], window[0][:])
         for a, b in SHARES:
             nc.scalar.activation(window[1][:].indirect(entries(place, a, b)), weighted[:, a:b], COPY)
-        weigh_and_scatter(1, LAST, S)
+        scatter(1, LAST, S)
         nc.sync.dma_start(out[P:, :], window[1][:])

@@ -26,8 +26,9 @@ HALF = S // 2
 FIRST = 384
 CLEARED = 3 * U // 4
 CUT = 512
-EDGES = (256, 512)
+EDGES = (256, 512, 768)
 LAST = 672
+STARTS = (0, CUT, 768)
 SHARES = ((0, 384), (384, LAST))
 
 
@@ -79,13 +80,13 @@ def tile_picked_route2_lingelu_p_kernel(tc, x_words, x_scales, gate, w1, offs, d
             acc = psum.tile([P, b - a], F32, name="acc%d_%d" % (blk, a))
             edges = [a] + [c for c in EDGES if a < c < b] + [b]
             for lo, hi in zip(edges, edges[1:]):
-                g = lo // CUT
+                g = max(lo // 256 - 1, 0)
                 h = lo // HALF
                 nc.tensor.matmul_mx(
                     out=acc[:, lo - a : hi - a],
                     lhsT=w_words[blk][:].bitcast(FP8X4),
                     lhsT_scale=w_scales[blk][:],
-                    rhs=picked_words[g][:, lo - g * CUT : hi - g * CUT].bitcast(FP8X4),
+                    rhs=picked_words[g][:, lo - STARTS[g] : hi - STARTS[g]].bitcast(FP8X4),
                     rhs_scale=plane[h][:, lo - h * HALF : hi - h * HALF],
                     start=True,
                     stop=True,
@@ -133,16 +134,18 @@ def tile_picked_route2_lingelu_p_kernel(tc, x_words, x_scales, gate, w1, offs, d
         )
         for a in (0, P // 2):
             quantise(0, a, a + P // 2)
-        picked_words.append(reuse.tile([P, S - CUT], U32, name="picked_words1", offset=4096, align_bytes=64))
-        w_bf.append(reuse.tile([P, P, PACK], BF16, name="w_bf1", offset=2048, align_bytes=64))
+        picked_words.append(reuse.tile([P, 256], U32, name="picked_words1", offset=1536, align_bytes=64))
+        nc.vector.tensor_copy(picked_words[1][:], words[:].indirect(entries(pick, CUT, 768)))
+        w_bf.append(keep.tile([P, P, PACK], BF16, name="w_bf1", align_bytes=64))
         interleave(w_bf[1][:, : P // 2, :], w_raw[:, :, : P // 2])
         nc.gpsimd.tensor_scalar(
             w_bf[1][:, P // 2 :, :], w_raw[:, :, P // 2 :].rearrange("p j m -> p m j"), 1.0, 0.0, MULT, ADD
         )
         quantise(1)
-        nc.vector.tensor_copy(picked_words[1][:], words[:].indirect(entries(pick, CUT, S)))
+        picked_words.append(reuse.tile([P, 256], U32, name="picked_words2", offset=4096, align_bytes=64))
+        nc.vector.tensor_copy(picked_words[2][:], words[:].indirect(entries(pick, 768, S)))
 
-        for blk, a, b in ((0, 0, 256), (1, 0, 384), (0, 256, HALF), (1, 384, 768), (0, HALF, S), (1, 768, S)):
+        for blk, a, b in ((0, 0, P), (0, P, 256), (1, 0, 384), (0, 256, HALF), (1, 384, 768), (0, HALF, S), (1, 768, S)):
             layer(blk, a, b)
         weighted = reuse.tile([P, LAST], F32, name="weighted", offset=8192, align_bytes=64)
         scatter(0, 0, 256)

@@ -27,9 +27,9 @@ FIRST = 384
 CLEARED = 3 * U // 4
 CUT = 512
 EDGES = (256, 512, 768)
-LAST = 672
+LAST = 704
 STARTS = (0, CUT, 768)
-SHARES = ((0, 384), (384, LAST))
+SHARES = ((0, 320), (320, LAST))
 
 
 def tile_picked_route2_lingelu_p_kernel(tc, x_words, x_scales, gate, w1, offs, dst, out):
@@ -145,7 +145,7 @@ def tile_picked_route2_lingelu_p_kernel(tc, x_words, x_scales, gate, w1, offs, d
         picked_words.append(reuse.tile([P, 256], U32, name="picked_words2", offset=4096, align_bytes=64))
         nc.vector.tensor_copy(picked_words[2][:], words[:].indirect(entries(pick, 768, S)))
 
-        for blk, a, b in ((0, 0, P), (0, P, 256), (1, 0, 384), (0, 256, HALF), (1, 384, 768), (0, HALF, S), (1, 768, S)):
+        for blk, a, b in ((0, 0, P), (0, P, 256), (0, 256, HALF), (1, 0, 384), (1, 384, 768), (0, HALF, S), (1, 768, S)):
             layer(blk, a, b)
         weighted = reuse.tile([P, LAST], F32, name="weighted", offset=8192, align_bytes=64)
         scatter(0, 0, 256)

@@ -26,10 +26,9 @@ HALF = S // 2
 FIRST = 384
 CLEARED = 3 * U // 4
 CUT = 512
-EDGES = (256, 512, 768)
 LAST = 704
-STARTS = (0, CUT, 768)
-SHARES = ((0, 320), (320, LAST))
+STARTS = (0, CUT, 896)
+SHARES = ((0, 384), (384, LAST))
 
 
 def tile_picked_route2_lingelu_p_kernel(tc, x_words, x_scales, gate, w1, offs, dst, out):
@@ -48,7 +47,7 @@ def tile_picked_route2_lingelu_p_kernel(tc, x_words, x_scales, gate, w1, offs, d
         zero = keep.tile([P, 1], F32, name="zero")
         w_pair = [
             keep.tile([P, 2, P], F32, name="w_pair0"),
-            reuse.tile([P, 2, P], F32, name="w_pair1", offset=1536, align_bytes=64),
+            reuse.tile([P, 2, P], F32, name="w_pair1", offset=1024, align_bytes=64),
         ]
         w_raw = reuse.tile([P, PACK, P], F32, name="w_raw", offset=4096, align_bytes=64)
         w_bf = [keep.tile([P, P, PACK], BF16, name="w_bf0", tag="w_bf0", align_bytes=64)]
@@ -57,7 +56,11 @@ def tile_picked_route2_lingelu_p_kernel(tc, x_words, x_scales, gate, w1, offs, d
             keep.tile([P, P], U32, name="w_words1", align_bytes=64),
         ]
         w_scales = [keep.tile([P, P], U8, name="w_scales%d" % b, align_bytes=64) for b in range(2)]
-        y = [keep.tile([P, S], F32, name="y%d" % b) for b in range(2)]
+        y0 = keep.tile([P, S], F32, name="y0")
+        y_share = [
+            keep.tile([P, 384], F32, name="y_share0"),
+            reuse.tile([P, LAST - 384], F32, name="y_share1", offset=12288, align_bytes=64),
+        ]
         window = [keep.tile([P, U], F32, name="window%d" % b) for b in range(2)]
         picked_words = [keep.tile([P, CUT], U32, name="picked_words0", align_bytes=64)]
 
@@ -76,11 +79,11 @@ def tile_picked_route2_lingelu_p_kernel(tc, x_words, x_scales, gate, w1, offs, d
                 in_=w_bf[blk][:, a:b, :].rearrange("p m j -> p (m j)"),
             )
 
-        def layer(blk, a, b):
+        def layer(blk, a, b, into, cuts):
             acc = psum.tile([P, b - a], F32, name="acc%d_%d" % (blk, a))
-            edges = [a] + [c for c in EDGES if a < c < b] + [b]
+            edges = [a] + [c for c in cuts if a < c < b] + [b]
             for lo, hi in zip(edges, edges[1:]):
-                g = max(lo // 256 - 1, 0)
+                g = sum(lo >= c for c in STARTS) - 1
                 h = lo // HALF
                 nc.tensor.matmul_mx(
                     out=acc[:, lo - a : hi - a],
@@ -91,10 +94,10 @@ def tile_picked_route2_lingelu_p_kernel(tc, x_words, x_scales, gate, w1, offs, d
                     start=True,
                     stop=True,
                 )
-            nc.scalar.activation(y[blk][:, a:b], acc[:], GELU)
+            nc.scalar.activation(into, acc[:], GELU)
 
-        def scatter(blk, a, b):
-            nc.vector.tensor_tensor(window[blk][:].indirect(entries(place, a, b)), y[blk][:, a:b], gates[:, a:b], MULT)
+        def scatter(blk, a, b, values):
+            nc.vector.tensor_tensor(window[blk][:].indirect(entries(place, a, b)), values, gates[:, a:b], MULT)
 
         x_flat = x_words[0].rearrange("p n t -> p (n t)").bitcast(I32)
         w_rows = w1.rearrange("(p j) m -> p j m", j=PACK)
@@ -134,26 +137,31 @@ def tile_picked_route2_lingelu_p_kernel(tc, x_words, x_scales, gate, w1, offs, d
         )
         for a in (0, P // 2):
             quantise(0, a, a + P // 2)
-        picked_words.append(reuse.tile([P, 256], U32, name="picked_words1", offset=1536, align_bytes=64))
-        nc.vector.tensor_copy(picked_words[1][:], words[:].indirect(entries(pick, CUT, 768)))
+        picked_words.append(reuse.tile([P, 384], U32, name="picked_words1", offset=1536, align_bytes=64))
+        nc.vector.tensor_copy(picked_words[1][:], words[:].indirect(entries(pick, CUT, 896)))
         w_bf.append(keep.tile([P, P, PACK], BF16, name="w_bf1", align_bytes=64))
         interleave(w_bf[1][:, : P // 2, :], w_raw[:, :, : P // 2])
         nc.gpsimd.tensor_scalar(
             w_bf[1][:, P // 2 :, :], w_raw[:, :, P // 2 :].rearrange("p j m -> p m j"), 1.0, 0.0, MULT, ADD
         )
         quantise(1)
-        picked_words.append(reuse.tile([P, 256], U32, name="picked_words2", offset=4096, align_bytes=64))
-        nc.vector.tensor_copy(picked_words[2][:], words[:].indirect(entries(pick, 768, S)))
+        picked_words.append(reuse.tile([P, P], U32, name="picked_words2", offset=4096, align_bytes=64))
+        nc.vector.tensor_copy(picked_words[2][:], words[:].indirect(entries(pick, 896, S)))
 
-        for blk, a, b in ((0, 0, P), (0, P, 256), (0, 256, HALF), (1, 0, 384), (1, 384, 768), (0, HALF, S), (1, 768, S)):
-            layer(blk, a, b)
+        for a, b in ((0, P), (P, 256), (256, HALF)):
+            layer(0, a, b, y0[:, a:b], ())
+        for values, (a, b) in zip(y_share, SHARES):
+            layer(1, a, b, values[:], (256, 512, 640))
+        layer(0, HALF, S, y0[:, HALF:], (768, 896))
         weighted = reuse.tile([P, LAST], F32, name="weighted", offset=8192, align_bytes=64)
-        scatter(0, 0, 256)
-        for a, b in SHARES:
-            nc.vector.tensor_tensor(weighted[:, a:b], y[1][:, a:b], gates[:, a:b], MULT)
-        scatter(0, 256, S)
+        scatter(0, 0, 256, y0[:, :256])
+        for values, (a, b) in zip(y_share, SHARES):
+            nc.vector.tensor_tensor(weighted[:, a:b], values[:], gates[:, a:b], MULT)
+        scatter(0, 256, S, y0[:, 256:])
         nc.sync.dma_start(out[:P, :], window[0][:])
-        for a, b in SHARES:
-            nc.scalar.activation(window[1][:].indirect(entries(place, a, b)), weighted[:, a:b], COPY)
-        scatter(1, LAST, S)
+        y_last = reuse.tile([P, S - LAST], F32, name="y_last", offset=12288, align_bytes=64)
+        nc.scalar.activation(window[1][:].indirect(entries(place, *SHARES[0])), weighted[:, :384], COPY)
+        layer(1, LAST, S, y_last[:], (768, 896))
+        nc.scalar.activation(window[1][:].indirect(entries(place, *SHARES[1])), weighted[:, 384:], COPY)
+        scatter(1, LAST, S, y_last[:])
         nc.sync.dma_start(out[P:, :], window[1][:])

@@ -28,7 +28,7 @@ CLEARED = 3 * U // 4
 CUT = 512
 LAST = 704
 STARTS = (0, CUT, 896)
-SHARES = ((0, 384), (384, LAST))
+SHARES = ((0, 320), (320, LAST))
 
 
 def tile_picked_route2_lingelu_p_kernel(tc, x_words, x_scales, gate, w1, offs, dst, out):
@@ -57,10 +57,7 @@ def tile_picked_route2_lingelu_p_kernel(tc, x_words, x_scales, gate, w1, offs, d
         ]
         w_scales = [keep.tile([P, P], U8, name="w_scales%d" % b, align_bytes=64) for b in range(2)]
         y0 = keep.tile([P, S], F32, name="y0")
-        y_share = [
-            keep.tile([P, 384], F32, name="y_share0"),
-            reuse.tile([P, LAST - 384], F32, name="y_share1", offset=12288, align_bytes=64),
-        ]
+        y1 = reuse.tile([P, LAST], F32, name="y1", offset=12288, align_bytes=64)
         window = [keep.tile([P, U], F32, name="window%d" % b) for b in range(2)]
         picked_words = [keep.tile([P, CUT], U32, name="picked_words0", align_bytes=64)]
 
@@ -150,18 +147,18 @@ def tile_picked_route2_lingelu_p_kernel(tc, x_words, x_scales, gate, w1, offs, d
 
         for a, b in ((0, P), (P, 256), (256, HALF)):
             layer(0, a, b, y0[:, a:b], ())
-        for values, (a, b) in zip(y_share, SHARES):
-            layer(1, a, b, values[:], (256, 512, 640))
+        for a, b in ((0, 384), (384, LAST)):
+            layer(1, a, b, y1[:, a:b], (256, 512, 640))
         layer(0, HALF, S, y0[:, HALF:], (768, 896))
         weighted = reuse.tile([P, LAST], F32, name="weighted", offset=8192, align_bytes=64)
         scatter(0, 0, 256, y0[:, :256])
-        for values, (a, b) in zip(y_share, SHARES):
-            nc.vector.tensor_tensor(weighted[:, a:b], values[:], gates[:, a:b], MULT)
+        for a, b in SHARES:
+            nc.vector.tensor_tensor(weighted[:, a:b], y1[:, a:b], gates[:, a:b], MULT)
         scatter(0, 256, S, y0[:, 256:])
         nc.sync.dma_start(out[:P, :], window[0][:])
         y_last = reuse.tile([P, S - LAST], F32, name="y_last", offset=12288, align_bytes=64)
-        nc.scalar.activation(window[1][:].indirect(entries(place, *SHARES[0])), weighted[:, :384], COPY)
+        nc.scalar.activation(window[1][:].indirect(entries(place, *SHARES[0])), weighted[:, :320], COPY)
         layer(1, LAST, S, y_last[:], (768, 896))
-        nc.scalar.activation(window[1][:].indirect(entries(place, *SHARES[1])), weighted[:, 384:], COPY)
+        nc.scalar.activation(window[1][:].indirect(entries(place, *SHARES[1])), weighted[:, 320:], COPY)
         scatter(1, LAST, S, y_last[:])
         nc.sync.dma_start(out[P:, :], window[1][:])

@@ -24,8 +24,9 @@ ROWS = 16
 BASE = P - ROWS
 HALF = S // 2
 FIRST = 384
+PLANES = ((0, 640), (640, S))
 CLEARED = 3 * U // 4
-CUT = 512
+CUT = 640
 LAST = 704
 STARTS = (0, CUT, 896)
 SHARES = ((0, 320), (320, LAST))
@@ -42,8 +43,8 @@ def tile_picked_route2_lingelu_p_kernel(tc, x_words, x_scales, gate, w1, offs, d
         place = keep.tile([P, S // LANES], U16, name="place")
         words = keep.tile([P, T], U32, name="words", align_bytes=64)
         scales = keep.tile([P, T], U8, name="scales", tag="table", align_bytes=64)
-        picked_scales = [keep.tile([P, HALF], U8, name="picked_scales%d" % h, align_bytes=64) for h in range(2)]
-        plane = [keep.tile([P, HALF], U8, name="plane%d" % h, align_bytes=64) for h in range(2)]
+        picked_scales = [keep.tile([P, b - a], U8, name="picked_scales%d" % a, align_bytes=64) for a, b in PLANES]
+        plane = [keep.tile([P, b - a], U8, name="plane%d" % a, align_bytes=64) for a, b in PLANES]
         zero = keep.tile([P, 1], F32, name="zero")
         w_pair = [
             keep.tile([P, 2, P], F32, name="w_pair0"),
@@ -81,13 +82,13 @@ def tile_picked_route2_lingelu_p_kernel(tc, x_words, x_scales, gate, w1, offs, d
             edges = [a] + [c for c in cuts if a < c < b] + [b]
             for lo, hi in zip(edges, edges[1:]):
                 g = sum(lo >= c for c in STARTS) - 1
-                h = lo // HALF
+                h = lo // PLANES[1][0]
                 nc.tensor.matmul_mx(
                     out=acc[:, lo - a : hi - a],
                     lhsT=w_words[blk][:].bitcast(FP8X4),
                     lhsT_scale=w_scales[blk][:],
                     rhs=picked_words[g][:, lo - STARTS[g] : hi - STARTS[g]].bitcast(FP8X4),
-                    rhs_scale=plane[h][:, lo - h * HALF : hi - h * HALF],
+                    rhs_scale=plane[h][:, lo - PLANES[h][0] : hi - PLANES[h][0]],
                     start=True,
                     stop=True,
                 )
@@ -120,7 +121,7 @@ def tile_picked_route2_lingelu_p_kernel(tc, x_words, x_scales, gate, w1, offs, d
                 )
 
         for h in range(2):
-            nc.vector.tensor_copy(picked_scales[h][:], scales[:].indirect(entries(pick, h * HALF, (h + 1) * HALF)))
+            nc.vector.tensor_copy(picked_scales[h][:], scales[:].indirect(entries(pick, *PLANES[h])))
         move_rows(nc.sync, 0)
         gates = keep.tile([P, S], F32, name="gates", tag="table", align_bytes=64)
         nc.sync.dma_start(gates[:, :FIRST], gate[:, :FIRST])
@@ -132,9 +133,8 @@ def tile_picked_route2_lingelu_p_kernel(tc, x_words, x_scales, gate, w1, offs, d
         nc.gpsimd.tensor_scalar(
             w_bf[0][:, P // 2 :, 2:4], w_pair[1][:, :, P // 2 :].rearrange("p j m -> p m j"), 1.0, 0.0, MULT, ADD
         )
-        for a in (0, P // 2):
-            quantise(0, a, a + P // 2)
-        picked_words.append(reuse.tile([P, 384], U32, name="picked_words1", offset=1536, align_bytes=64))
+        quantise(0)
+        picked_words.append(reuse.tile([P, 256], U32, name="picked_words1", offset=1536, align_bytes=64))
         nc.vector.tensor_copy(picked_words[1][:], words[:].indirect(entries(pick, CUT, 896)))
         w_bf.append(keep.tile([P, P, PACK], BF16, name="w_bf1", align_bytes=64))
         interleave(w_bf[1][:, : P // 2, :], w_raw[:, :, : P // 2])
@@ -145,11 +145,11 @@ def tile_picked_route2_lingelu_p_kernel(tc, x_words, x_scales, gate, w1, offs, d
         picked_words.append(reuse.tile([P, P], U32, name="picked_words2", offset=4096, align_bytes=64))
         nc.vector.tensor_copy(picked_words[2][:], words[:].indirect(entries(pick, 896, S)))
 
-        for a, b in ((0, P), (P, 256), (256, HALF)):
-            layer(0, a, b, y0[:, a:b], ())
+        for a, b in ((0, P), (P, 256), (256, CUT)):
+            layer(0, a, b, y0[:, a:b], (HALF,))
         for a, b in ((0, 384), (384, LAST)):
-            layer(1, a, b, y1[:, a:b], (256, 512, 640))
-        layer(0, HALF, S, y0[:, HALF:], (768, 896))
+            layer(1, a, b, y1[:, a:b], (256, 640))
+        layer(0, CUT, S, y0[:, CUT:], (896,))
         weighted = reuse.tile([P, LAST], F32, name="weighted", offset=8192, align_bytes=64)
         scatter(0, 0, 256, y0[:, :256])
         for a, b in SHARES:

@@ -24,9 +24,9 @@ ROWS = 16
 BASE = P - ROWS
 HALF = S // 2
 FIRST = 384
-PLANES = ((0, 640), (640, S))
+PLANES = ((0, 576), (576, S))
 CLEARED = 3 * U // 4
-CUT = 640
+CUT = 576
 LAST = 704
 STARTS = (0, CUT, 896)
 SHARES = ((0, 320), (320, LAST))
@@ -134,7 +134,7 @@ def tile_picked_route2_lingelu_p_kernel(tc, x_words, x_scales, gate, w1, offs, d
             w_bf[0][:, P // 2 :, 2:4], w_pair[1][:, :, P // 2 :].rearrange("p j m -> p m j"), 1.0, 0.0, MULT, ADD
         )
         quantise(0)
-        picked_words.append(reuse.tile([P, 256], U32, name="picked_words1", offset=1536, align_bytes=64))
+        picked_words.append(reuse.tile([P, 896 - CUT], U32, name="picked_words1", offset=1536, align_bytes=64))
         nc.vector.tensor_copy(picked_words[1][:], words[:].indirect(entries(pick, CUT, 896)))
         w_bf.append(keep.tile([P, P, PACK], BF16, name="w_bf1", align_bytes=64))
         interleave(w_bf[1][:, : P // 2, :], w_raw[:, :, : P // 2])
@@ -148,8 +148,8 @@ def tile_picked_route2_lingelu_p_kernel(tc, x_words, x_scales, gate, w1, offs, d
         for a, b in ((0, P), (P, 256), (256, CUT)):
             layer(0, a, b, y0[:, a:b], (HALF,))
         for a, b in ((0, 384), (384, LAST)):
-            layer(1, a, b, y1[:, a:b], (256, 640))
-        layer(0, CUT, S, y0[:, CUT:], (896,))
+            layer(1, a, b, y1[:, a:b], (256, HALF, CUT))
+        layer(0, CUT, S, y0[:, CUT:], (832, 896))
         weighted = reuse.tile([P, LAST], F32, name="weighted", offset=8192, align_bytes=64)
         scatter(0, 0, 256, y0[:, :256])
         for a, b in SHARES:

@@ -41,16 +41,16 @@ def tile_picked_route2_lingelu_p_kernel(tc, x_words, x_scales, gate, w1, offs, d
 
         pick = keep.tile([P, S // LANES], U16, name="pick")
         place = keep.tile([P, S // LANES], U16, name="place")
-        words = keep.tile([P, T], U32, name="words", align_bytes=64)
-        scales = keep.tile([P, T], U8, name="scales", tag="table", align_bytes=64)
+        words = keep.tile([P, T], U32, name="words", align_bytes=256)
+        scales = keep.tile([P, T], U8, name="scales", tag="table", align_bytes=256)
         picked_scales = [keep.tile([P, b - a], U8, name="picked_scales%d" % a, align_bytes=64) for a, b in PLANES]
         plane = [keep.tile([P, b - a], U8, name="plane%d" % a, align_bytes=64) for a, b in PLANES]
         zero = keep.tile([P, 1], F32, name="zero")
         w_pair = [
-            keep.tile([P, 2, P], F32, name="w_pair0"),
-            reuse.tile([P, 2, P], F32, name="w_pair1", offset=1024, align_bytes=64),
+            keep.tile([P, 2, P], F32, name="w_pair0", align_bytes=256),
+            reuse.tile([P, 2, P], F32, name="w_pair1", offset=1024, align_bytes=256),
         ]
-        w_raw = reuse.tile([P, PACK, P], F32, name="w_raw", offset=4096, align_bytes=64)
+        w_raw = reuse.tile([P, PACK, P], F32, name="w_raw", offset=4096, align_bytes=256)
         w_bf = [keep.tile([P, P, PACK], BF16, name="w_bf0", tag="w_bf0", align_bytes=64)]
         w_words = [
             reuse.tile([P, P], U32, name="w_words0", offset=8192, align_bytes=64),
@@ -59,7 +59,7 @@ def tile_picked_route2_lingelu_p_kernel(tc, x_words, x_scales, gate, w1, offs, d
         w_scales = [keep.tile([P, P], U8, name="w_scales%d" % b, align_bytes=64) for b in range(2)]
         y0 = keep.tile([P, S], F32, name="y0")
         y1 = reuse.tile([P, LAST], F32, name="y1", offset=12288, align_bytes=64)
-        window = [keep.tile([P, U], F32, name="window%d" % b) for b in range(2)]
+        window = [keep.tile([P, U], F32, name="window%d" % b, align_bytes=256) for b in range(2)]
         picked_words = [keep.tile([P, CUT], U32, name="picked_words0", align_bytes=64)]
 
         def entries(tile, a, b):
@@ -123,7 +123,7 @@ def tile_picked_route2_lingelu_p_kernel(tc, x_words, x_scales, gate, w1, offs, d
         for h in range(2):
             nc.vector.tensor_copy(picked_scales[h][:], scales[:].indirect(entries(pick, *PLANES[h])))
         move_rows(nc.sync, 0)
-        gates = keep.tile([P, S], F32, name="gates", tag="table", align_bytes=64)
+        gates = keep.tile([P, S], F32, name="gates", tag="table", align_bytes=256)
         nc.sync.dma_start(gates[:, :FIRST], gate[:, :FIRST])
         move_rows(nc.sync, 1)
         nc.sync.dma_start(gates[:, FIRST:], gate[:, FIRST:])

from contextlib import ExitStack

import concourse.mybir as mybir

K, T, S, N, U = 512, 2048, 1024, 256, 2048
FLOPS = 2 * K * N * S

F32 = mybir.dt.float32
BF16 = mybir.dt.bfloat16
I32 = mybir.dt.int32
U32 = mybir.dt.uint32
U16 = mybir.dt.uint16
U8 = mybir.dt.uint8
FP8X4 = mybir.dt.float8_e4m3fn_x4
GELU = mybir.ActivationFunctionType.Gelu_apprx_tanh
COPY = mybir.ActivationFunctionType.Copy
MULT = mybir.AluOpType.mult
ADD = mybir.AluOpType.add

P = 128
PACK = 4
LANES = 16
ROWS = 16
BASE = P - ROWS
HALF = S // 2
FIRST = 384
PLANES = ((0, 576), (576, S))
CLEARED = 3 * U // 4
CUT = 576
LAST = 704
STARTS = (0, CUT, 896)
SHARES = ((0, 320), (320, LAST))


def tile_picked_route2_lingelu_p_kernel(tc, x_words, x_scales, gate, w1, offs, dst, out):
    nc = tc.nc
    with ExitStack() as ctx:
        keep = ctx.enter_context(tc.tile_pool(name="keep", bufs=1))
        reuse = ctx.enter_context(tc.tile_pool(name="reuse", bufs=1))
        psum = ctx.enter_context(tc.psum_pool(name="psum", bufs=1))

        pick = keep.tile([P, S // LANES], U16, name="pick")
        place = keep.tile([P, S // LANES], U16, name="place")
        words = keep.tile([P, T], U32, name="words", align_bytes=256)
        scales = keep.tile([P, T], U8, name="scales", tag="table", align_bytes=256)
        picked_scales = [keep.tile([P, b - a], U8, name="picked_scales%d" % a, align_bytes=64) for a, b in PLANES]
        plane = [keep.tile([P, b - a], U8, name="plane%d" % a, align_bytes=64) for a, b in PLANES]
        zero = keep.tile([P, 1], F32, name="zero")
        w_pair = [
            keep.tile([P, 2, P], F32, name="w_pair0", align_bytes=256),
            reuse.tile([P, 2, P], F32, name="w_pair1", offset=1024, align_bytes=256),
        ]
        w_raw = reuse.tile([P, PACK, P], F32, name="w_raw", offset=4096, align_bytes=256)
        w_bf = [keep.tile([P, P, PACK], BF16, name="w_bf0", tag="w_bf0", align_bytes=64)]
        w_words = [
            reuse.tile([P, P], U32, name="w_words0", offset=8192, align_bytes=64),
            keep.tile([P, P], U32, name="w_words1", align_bytes=64),
        ]
        w_scales = [keep.tile([P, P], U8, name="w_scales%d" % b, align_bytes=64) for b in range(2)]
        y0 = keep.tile([P, S], F32, name="y0")
        y1 = reuse.tile([P, LAST], F32, name="y1", offset=12288, align_bytes=64)
        window = [keep.tile([P, U], F32, name="window%d" % b, align_bytes=256) for b in range(2)]
        picked_words = [keep.tile([P, CUT], U32, name="picked_words0", align_bytes=64)]

        def entries(tile, a, b):
            return tile[:, a // LANES : b // LANES]

        def interleave(grouped, rows):
            nc.scalar.copy(
                grouped.rearrange("p (c i) j -> p c j i", i=4), rows.rearrange("p j (c i) -> p c j i", i=4)
            )

        def quantise(blk, a=0, b=P):
            nc.vector.quantize_mx(
                out=w_words[blk][:, a:b].bitcast(FP8X4),
                scales=w_scales[blk][:, a:b],
                in_=w_bf[blk][:, a:b, :].rearrange("p m j -> p (m j)"),
            )

        def layer(blk, a, b, into, cuts):
            acc = psum.tile([P, b - a], F32, name="acc%d_%d" % (blk, a))
            edges = [a] + [c for c in cuts if a < c < b] + [b]
            for lo, hi in zip(edges, edges[1:]):
                g = sum(lo >= c for c in STARTS) - 1
                h = lo // PLANES[1][0]
                nc.tensor.matmul_mx(
                    out=acc[:, lo - a : hi - a],
                    lhsT=w_words[blk][:].bitcast(FP8X4),
                    lhsT_scale=w_scales[blk][:],
                    rhs=picked_words[g][:, lo - STARTS[g] : hi - STARTS[g]].bitcast(FP8X4),
                    rhs_scale=plane[h][:, lo - PLANES[h][0] : hi - PLANES[h][0]],
                    start=True,
                    stop=True,
                )
            nc.scalar.activation(into, acc[:], GELU)

        def scatter(blk, a, b, values):
            nc.vector.tensor_tensor(window[blk][:].indirect(entries(place, a, b)), values, gates[:, a:b], MULT)

        x_flat = x_words[0].rearrange("p n t -> p (n t)").bitcast(I32)
        w_rows = w1.rearrange("(p j) m -> p j m", j=PACK)
        nc.scalar.dma_start(scales[BASE:P, :].bitcast(I32), x_scales[0].bitcast(I32))
        nc.sync.dma_start(pick[:], offs)
        nc.sync.dma_start(words[:].bitcast(I32), x_flat)
        for u in range(2):
            nc.sync.dma_start(w_pair[u][:], w_rows[:, 2 * u : 2 * u + 2, :P])
        nc.sync.dma_start(w_raw[:], w_rows[:, :, P:])
        nc.sync.dma_start(place[:], dst)

        nc.vector.memset(zero[:], 0.0)
        nc.vector.memset(scales[0:BASE, :].bitcast(I32), 0)
        nc.vector.memset(window[0][:, :CLEARED], 0.0)
        nc.scalar.activation(window[0][:, CLEARED:], zero[:].to_broadcast([P, U - CLEARED]), GELU)
        nc.scalar.activation(window[1][:], zero[:].to_broadcast([P, U]), GELU)

        def move_rows(queue, h):
            for r in range(4):
                queue.dma_start(
                    plane[h][r:P:32, :].bitcast(I32),
                    picked_scales[h][BASE + r : P : 4, :].bitcast(I32),
                )

        for h in range(2):
            nc.vector.tensor_copy(picked_scales[h][:], scales[:].indirect(entries(pick, *PLANES[h])))
        move_rows(nc.sync, 0)
        gates = keep.tile([P, S], F32, name="gates", tag="table", align_bytes=256)
        nc.sync.dma_start(gates[:, :FIRST], gate[:, :FIRST])
        move_rows(nc.sync, 1)
        nc.sync.dma_start(gates[:, FIRST:], gate[:, FIRST:])
        nc.vector.tensor_copy(picked_words[0][:], words[:].indirect(entries(pick, 0, CUT)))
        interleave(w_bf[0][:, :, 0:2], w_pair[0][:])
        interleave(w_bf[0][:, : P // 2, 2:4], w_pair[1][:, :, : P // 2])
        nc.gpsimd.tensor_scalar(
            w_bf[0][:, P // 2 :, 2:4], w_pair[1][:, :, P // 2 :].rearrange("p j m -> p m j"), 1.0, 0.0, MULT, ADD
        )
        quantise(0)
        picked_words.append(reuse.tile([P, 896 - CUT], U32, name="picked_words1", offset=1536, align_bytes=64))
        nc.vector.tensor_copy(picked_words[1][:], words[:].indirect(entries(pick, CUT, 896)))
        w_bf.append(keep.tile([P, P, PACK], BF16, name="w_bf1", align_bytes=64))
        interleave(w_bf[1][:, : P // 2, :], w_raw[:, :, : P // 2])
        nc.gpsimd.tensor_scalar(
            w_bf[1][:, P // 2 :, :], w_raw[:, :, P // 2 :].rearrange("p j m -> p m j"), 1.0, 0.0, MULT, ADD
        )
        quantise(1)
        picked_words.append(reuse.tile([P, P], U32, name="picked_words2", offset=4096, align_bytes=64))
        nc.vector.tensor_copy(picked_words[2][:], words[:].indirect(entries(pick, 896, S)))

        for a, b in ((0, P), (P, 256), (256, CUT)):
            layer(0, a, b, y0[:, a:b], (HALF,))
        for a, b in ((0, 384), (384, LAST)):
            layer(1, a, b, y1[:, a:b], (256, HALF, CUT))
        layer(0, CUT, S, y0[:, CUT:], (832, 896))
        weighted = reuse.tile([P, LAST], F32, name="weighted", offset=8192, align_bytes=64)
        scatter(0, 0, 256, y0[:, :256])
        for a, b in SHARES:
            nc.vector.tensor_tensor(weighted[:, a:b], y1[:, a:b], gates[:, a:b], MULT)
        scatter(0, 256, S, y0[:, 256:])
        nc.sync.dma_start(out[:P, :], window[0][:])
        y_last = reuse.tile([P, S - LAST], F32, name="y_last", offset=12288, align_bytes=64)
        nc.scalar.activation(window[1][:].indirect(entries(place, *SHARES[0])), weighted[:, :320], COPY)
        layer(1, LAST, S, y_last[:], (768, 896))
        nc.scalar.activation(window[1][:].indirect(entries(place, *SHARES[1])), weighted[:, 320:], COPY)
        scatter(1, LAST, S, y_last[:])
        nc.sync.dma_start(out[P:, :], window[1][:])
